import numpy as np
import ml_dtypes


def mxq(x, axis, fmt="e4m3"):
    dtype, down = {"e4m3": (ml_dtypes.float8_e4m3fn, 7), "e5m2": (ml_dtypes.float8_e5m2, 14)}[fmt]
    v = np.moveaxis(np.asarray(x, np.float32).astype(ml_dtypes.bfloat16).astype(np.float64), axis, -1)
    blocks = v.reshape(v.shape[:-1] + (-1, 32))
    amax = np.abs(blocks).max(-1, keepdims=True)
    byte = np.maximum(np.where(amax > 0, np.frexp(amax)[1] - 1 + 127, 0) - down, 1)
    scale = np.exp2(byte - 127.0)
    codes = (blocks / scale).astype(np.float32).astype(dtype).astype(np.float64)
    return np.moveaxis((codes * scale).reshape(v.shape), -1, axis)


WIDE = False


def mx_kscale(k):
    if not WIDE:
        return np.ones(k)
    levels = np.array([10, -10, 5, -5, 0])
    if k % 512:
        return np.exp2(np.random.permutation(np.resize(levels, k // 32))).repeat(32)
    a = np.empty((k // 512, 16))
    for p in range(k // 512):
        a[p, :8] = np.random.permutation(np.resize(levels, 8))
        for g in range(8):
            far = levels[np.abs(levels - a[p, g]) >= 10]
            a[p, g + 8] = far[np.random.randint(len(far))]
    return np.exp2(a.ravel()).repeat(32)


def f64(x):
    return np.asarray(x).astype(np.float64)


def striped(idx):
    return np.tile(idx.reshape(-1, 16).T, (8, 1)).astype(np.uint16)


def unstriped(offs):
    return offs[:16].T.reshape(-1).astype(np.int64)


E2M1 = np.array([0.0, 0.5, 1.0, 1.5, 2.0, 3.0, 4.0, 6.0, -0.0, -0.5, -1.0, -1.5, -2.0, -3.0, -4.0, -6.0])


def pack_weight(w, fmt):
    k, n = w.shape
    w = f64(np.asarray(w, np.float32).astype(ml_dtypes.bfloat16)).reshape(k // 32, 32, n)
    amax = np.abs(w).max(1)
    if fmt == "e4m3":
        byte = np.frexp(amax)[1] - 1 + 127 - 7
    else:
        mant, ex = np.frexp(amax / 6.0)
        byte = np.where(mant > 0.5, ex, ex - 1) + 127
    byte = np.clip(np.where(amax > 0, byte, 1), 1, 254)
    scaled = (w * np.exp2(127.0 - byte)[:, None, :]).reshape(k, n).astype(np.float32)
    by_word = np.ascontiguousarray(scaled.reshape(k // 512, 128, 4, n).transpose(0, 1, 3, 2))
    if fmt == "e4m3":
        words = by_word.astype(ml_dtypes.float8_e4m3fn).view(np.uint8)
    else:
        c = by_word.astype(ml_dtypes.float4_e2m1fn).view(np.uint8) & 0xF
        words = (c[..., 0::2] | (c[..., 1::2] << 4)).reshape(k // 512, 128, 2 * n)
    return np.ascontiguousarray(words), np.ascontiguousarray(byte.astype(np.uint8).reshape(k // 512, 16, n))


def unpack_weight(words, scales, fmt):
    g, _, n = scales.shape
    words = np.ascontiguousarray(words).reshape(g, 128, n, -1)
    if fmt == "e4m3":
        vals = words.view(ml_dtypes.float8_e4m3fn).astype(np.float64)
    else:
        nib = np.empty((g, 128, n, 4), np.uint8)
        nib[..., 0::2] = words & 0xF
        nib[..., 1::2] = words >> 4
        vals = E2M1[nib]
    vals = vals * np.repeat(np.exp2(scales.astype(np.float64) - 127.0), 8, axis=1)[..., None]
    return vals.transpose(0, 1, 3, 2).reshape(g * 512, n)


def gelu(v):
    return 0.5 * v * (1.0 + np.tanh(np.sqrt(2.0 / np.pi) * (v + 0.044715 * v**3)))


def often(T, S):
    return np.random.permutation(T)[(T * np.random.uniform(0, 1, S) ** 4).astype(np.int64)]


K, K2, H, N, T, S = 512, 1024, 1024, 512, 4096, 1024

def setup_inputs():
    n = np.random.standard_normal
    s = mx_kscale(K)[:, None]
    s2 = mx_kscale(K2)[:, None]
    u = mx_kscale(H)[:, None]
    tab_words, tab_scales = pack_weight(n((K, T)) * s, "e4m3")
    tab2_words, tab2_scales = pack_weight(n((K2, T)) * s2, "e2m1")
    w4_words, w4_scales = pack_weight(n((K, H)) / np.sqrt(K) / s * u.T, "e2m1")
    w8_words, w8_scales = pack_weight(n((H, N)) / np.sqrt(H) / u, "e4m3")
    return {
        "tab_words": tab_words, "tab_scales": tab_scales,
        "tab2_words": tab2_words, "tab2_scales": tab2_scales,
        "offs": striped(often(T, S)),
        "offs2": striped(often(T, S)),
        "w4_words": w4_words, "w4_scales": w4_scales,
        "w2": (n((K2, H)) / np.sqrt(K2) / s2 * u.T).astype(np.float32),
        "w8_words": w8_words, "w8_scales": w8_scales,
        "tw": np.exp(0.4 * n((N, S))).astype(np.float32),
    }

def reference(tab_words, tab_scales, tab2_words, tab2_scales, offs, offs2,
              w4_words, w4_scales, w2, w8_words, w8_scales, tw):
    v = unpack_weight(tab_words, tab_scales, "e4m3")[:, unstriped(offs)]
    v2 = unpack_weight(tab2_words, tab2_scales, "e2m1")[:, unstriped(offs2)]
    w4 = unpack_weight(w4_words, w4_scales, "e2m1")
    scan = w4.T @ v
    old = mxq(f64(w2), 0, "e4m3").T @ v2
    gap = np.maximum(scan, old) - np.minimum(scan, old)
    w8 = unpack_weight(w8_words, w8_scales, "e4m3")
    y = w8.T @ mxq(gap, 0, "e4m3")
    return np.abs(y) * f64(tw)

@@ -1,0 +1,199 @@
+from contextlib import ExitStack
+
+import concourse.mybir as mybir
+
+K, K2, H, N, T, S = 512, 1024, 1024, 512, 4096, 1024
+FLOPS = 2 * S * (K * H + K2 * H + H * N)
+
+F32 = mybir.dt.float32
+BF16 = mybir.dt.bfloat16
+I32 = mybir.dt.int32
+U32 = mybir.dt.uint32
+U16 = mybir.dt.uint16
+U8 = mybir.dt.uint8
+FP8X4 = mybir.dt.float8_e4m3fn_x4
+FP4X4 = mybir.dt.float4_e2m1fn_x4
+ALU = mybir.AluOpType
+ABS = mybir.ActivationFunctionType.Abs
+
+P = 128
+PACK = 4
+KP = P * PACK
+HALF = S // 2
+CH = 128
+NCH = S // CH
+FIN = 256
+
+
+def tile_list_map_change_gap_kernel(tc, tab_words, tab_scales, tab2_words, tab2_scales, offs, offs2,
+                                              w4_words, w4_scales, w2, w8_words, w8_scales, tw, out):
+    nc = tc.nc
+    with ExitStack() as ctx:
+        keep = ctx.enter_context(tc.tile_pool(name="keep", bufs=1))
+        psum = ctx.enter_context(tc.psum_pool(name="psum", bufs=1))
+
+        def sb(name, shape, dtype):
+            return keep.tile(shape, dtype, name=name, align_bytes=64)
+
+        def ring(name, shape, dtype, bufs):
+            return keep.tile(shape, dtype, name=name, tag=name, bufs=bufs, align_bytes=64)
+
+        list1 = keep.tile([P, S // 16], U16, name="list1")
+        list2 = keep.tile([P, S // 16], U16, name="list2")
+        def staged(slot, name, shape, dtype):
+            return keep.tile(shape, dtype, name=name, tag=slot, bufs=1, align_bytes=64)
+
+        def w2_tile(b, a, slot):
+            w2_raw[b, a] = staged(slot, "w2_raw%d%d" % (b, a), [P, PACK, KP], F32)
+            nc.sync.dma_start(w2_raw[b, a][:],
+                              w2[KP * a:KP * (a + 1), KP * b:KP * (b + 1)].rearrange("(p j) c -> p j c", j=PACK))
+
+        def load_tab2(a, slot):
+            tab2_w[a] = staged(slot, "tab2_w%d" % a, [P, T], U16)
+            nc.sync.dma_start(tab2_w[a][:].bitcast(I32), tab2_words[a].bitcast(I32))
+
+        def load_tw(u, slot):
+            tw_sb[u] = staged(slot, "tw%d" % u, [P, N // P, HALF], F32)
+            nc.sync.dma_start(tw_sb[u][:], tw[:, HALF * u:HALF * (u + 1)].rearrange("(nt p) s -> p nt s", p=P))
+
+        def load_scales(clear, queue, plane, scales):
+            rows = 4 * scales.shape[0]
+            clear.memset(plane[:].bitcast(I32), 0)
+            for q in range(4):
+                queue.dma_start(plane[32 * q:32 * q + rows, :].bitcast(I32), scales[:, 4 * q:4 * q + 4, :].bitcast(I32))
+
+        def permute_w4(dst, src):
+            nc.vector.tensor_copy(dst[:].rearrange("p (b t m) -> p b m t", b=2, t=PACK),
+                                  src[:].rearrange("p (b m t) -> p b m t", b=2, t=PACK))
+
+        w2_raw, tab2_w, tw_sb = {}, {}, {}
+        nc.sync.dma_start(list2[:], offs2)
+        nc.sync.dma_start(list1[:], offs)
+        w4_raw = staged("slot_c", "w4_raw", [P, H], U16)
+        nc.sync.dma_start(w4_raw[:].bitcast(I32), w4_words[0].bitcast(I32))
+        w4_sc_raw = staged("slot_e", "w4_sc_raw", [P, H], U8)
+        load_scales(nc.vector, nc.gpsimd, w4_sc_raw, w4_scales)
+        tab2_sc = staged("slot_a", "tab2_sc", [P, T], U8)
+        load_scales(nc.vector, nc.scalar, tab2_sc, tab2_scales)
+        tab_sc = staged("slot_b", "tab_sc", [P, T], U8)
+        load_scales(nc.vector, nc.scalar, tab_sc, tab_scales)
+        w2_tile(0, 0, "slot_f")
+        w2_tile(0, 1, "slot_g")
+        v2_sc1 = sb("v2_sc1", [P, S], U8)
+        nc.vector.memset(v2_sc1[:].bitcast(I32), 0)
+
+        w4_w = sb("w4_w", [P, H], U16)
+        permute_w4(w4_w, w4_raw)
+        tab_w = staged("slot_c", "tab_w", [P, T], U32)
+        nc.sync.dma_start(tab_w[:].bitcast(I32), tab_words[0].rearrange("p t i -> p (t i)").bitcast(I32))
+
+        v2_sc0 = sb("v2_sc0", [P, S], U8)
+        nc.vector.tensor_copy(v2_sc0[:], tab2_sc[:].indirect(list2[:]))
+        for q in range(4):
+            nc.gpsimd.dma_start(v2_sc1[32 * q:32 * q + 4, :].bitcast(I32), v2_sc0[32 * q + 4:32 * q + 8, :].bitcast(I32))
+        v2_sc = [v2_sc0, v2_sc1]
+        v_sc = sb("v_sc", [P, S], U8)
+        nc.vector.tensor_copy(v_sc[:], tab_sc[:].indirect(list1[:]))
+        w4_sc = staged("slot_b", "w4_sc", [P, H], U8)
+        permute_w4(w4_sc, w4_sc_raw)
+        w8_sc = staged("slot_e", "w8_sc", [P, N], U8)
+        load_scales(nc.vector, nc.sync, w8_sc, w8_scales)
+
+        w2_codes, w2_sc = {}, {}
+
+        def quantise_w2(b, a, copy):
+            grouped = sb("w2_bf%d%d" % (b, a), [P, PACK * KP], BF16)
+            copy(grouped[:].rearrange("p (t m j) -> p m j t", t=PACK, j=PACK),
+                 w2_raw[b, a][:].rearrange("p j (m t) -> p m j t", t=PACK))
+            w2_codes[b, a] = sb("w2_codes%d%d" % (b, a), [P, KP], U32)
+            w2_sc[b, a] = sb("w2_sc%d%d" % (b, a), [P, KP], U8)
+            nc.vector.quantize_mx(out=w2_codes[b, a][:].bitcast(FP8X4), scales=w2_sc[b, a][:], in_=grouped[:])
+
+        def gather_half(name, dtype, window, offsets, h):
+            picked = sb(name, [P, HALF], dtype)
+            nc.vector.tensor_copy(picked[:], window[:].indirect(offsets[:, h * HALF // 16:(h + 1) * HALF // 16]))
+            return picked
+
+        quantise_w2(0, 0, nc.scalar.copy)
+        load_tab2(0, "slot_f")
+        quantise_w2(0, 1, nc.scalar.copy)
+        load_tab2(1, "slot_g")
+        v_w = [gather_half("v_w%d" % h, U32, tab_w, list1, h) for h in range(2)]
+        w2_tile(1, 0, "slot_c")
+        v2_w = {(0, h): gather_half("v2_w0%d" % h, U16, tab2_w[0], list2, h) for h in range(2)}
+        w2_tile(1, 1, "slot_f")
+        for h in range(2):
+            v2_w[1, h] = gather_half("v2_w1%d" % h, U16, tab2_w[1], list2, h)
+        load_tw(0, "slot_g")
+        quantise_w2(1, 0, nc.scalar.copy)
+        w8_w = staged("slot_c", "w8_w", [P, 2 * N], U32)
+        nc.sync.dma_start(w8_w[:].bitcast(I32).rearrange("p (b c) -> p b c", b=2),
+                          w8_words.rearrange("b p c i -> p b (c i)").bitcast(I32))
+        quantise_w2(1, 1, nc.vector.tensor_copy)
+        load_tw(1, "slot_f")
+
+        scan_sb, diff = {}, {}
+
+        def scan_chunk(b, c):
+            h, col = divmod(c * CH, HALF)
+            acc = psum.tile([P, PACK, CH], F32, name="scan_ps", tag="scan_ps", bufs=2)
+            for t in range(PACK):
+                cols = slice(KP * b + P * t, KP * b + P * (t + 1))
+                nc.tensor.matmul_mx(out=acc[:, t, :], lhsT=w4_w[:, cols].bitcast(FP4X4), lhsT_scale=w4_sc[:, cols],
+                                    rhs=v_w[h][:, col:col + CH].bitcast(FP8X4), rhs_scale=v_sc[:, c * CH:(c + 1) * CH],
+                                    start=True, stop=True)
+            scan_sb[b, c] = sb("scan%d%d" % (b, c), [P, CH, PACK], F32)
+            nc.scalar.copy(scan_sb[b, c][:], acc[:].rearrange("p t s -> p s t"))
+
+        def old_chunk(b, c):
+            h, col = divmod(c * CH, HALF)
+            acc = psum.tile([P, PACK, CH], F32, name="old_ps", tag="old_ps", bufs=4)
+            for t in range(PACK):
+                cols = slice(P * t, P * (t + 1))
+                for a in range(2):
+                    nc.tensor.matmul_mx(out=acc[:, t, :], lhsT=w2_codes[b, a][:, cols].bitcast(FP8X4),
+                                        lhsT_scale=w2_sc[b, a][:, cols],
+                                        rhs=v2_w[a, h][:, col:col + CH].bitcast(FP4X4),
+                                        rhs_scale=v2_sc[a][:, c * CH:(c + 1) * CH], start=(a == 0), stop=(a == 1))
+            diff[b, c] = sb("diff%d%d" % (b, c), [P, CH, PACK], BF16)
+            nc.vector.tensor_tensor(diff[b, c][:], acc[:].rearrange("p t s -> p s t"), scan_sb[b, c][:], ALU.subtract)
+
+        gap_codes, gap_sc = {}, {}
+
+        def gap_piece(b, f):
+            gap = ring("gap", [P, FIN * PACK], BF16, 4)
+            for i in range(FIN // CH):
+                nc.scalar.activation(gap[:, i * CH * PACK:(i + 1) * CH * PACK],
+                                     diff[b, f * (FIN // CH) + i][:].rearrange("p s t -> p (s t)"), ABS)
+            gap_codes[b, f] = sb("gap_codes%d%d" % (b, f), [P, FIN], U32)
+            gap_sc[b, f] = sb("gap_sc%d%d" % (b, f), [P, FIN], U8)
+            nc.vector.quantize_mx(out=gap_codes[b, f][:].bitcast(FP8X4), scales=gap_sc[b, f][:], in_=gap[:])
+
+        def final_piece(f):
+            for g in range(2):
+                acc = psum.tile([P, 2, FIN], F32, name="y_ps", tag="y_ps", bufs=2)
+                for i in range(2):
+                    cols = slice(P * (2 * g + i), P * (2 * g + i + 1))
+                    for b in range(2):
+                        nc.tensor.matmul_mx(out=acc[:, i, :], lhsT=w8_w[:, N * b + cols.start:N * b + cols.stop].bitcast(FP8X4),
+                                            lhsT_scale=w8_sc[4 * b:P, cols], rhs=gap_codes[b, f][:].bitcast(FP8X4),
+                                            rhs_scale=gap_sc[b, f][:], start=(b == 0), stop=(b == 1))
+                weighted = ring("weighted", [P, 2, FIN], F32, 3)
+                nc.vector.tensor_tensor(weighted[:], acc[:], tw_sb[f // 2][:, 2 * g:2 * g + 2, FIN * (f % 2):FIN * (f % 2 + 1)], ALU.mult)
+                res = ring("res", [P, 2, FIN], F32, 4)
+                nc.scalar.activation(res[:], weighted[:], ABS)
+                nc.sync.dma_start(
+                    out[2 * P * g:2 * P * (g + 1), FIN * f:FIN * (f + 1)].rearrange("(i p) s -> p i s", p=P), res[:])
+
+        for c in range(NCH):
+            scan_chunk(0, c)
+        for c in range(NCH):
+            old_chunk(0, c)
+        for c in range(NCH):
+            scan_chunk(1, c)
+        for f in range(S // FIN):
+            for i in range(FIN // CH):
+                old_chunk(1, f * (FIN // CH) + i)
+            gap_piece(0, f)
+            gap_piece(1, f)
+            final_piece(f)

@@ -69,40 +69,35 @@ def tile_list_map_change_gap_kernel(tc, tab_words, tab_scales, tab2_words, tab2_
         w2_raw, tab2_w, tw_sb = {}, {}, {}
         nc.sync.dma_start(list2[:], offs2)
         nc.sync.dma_start(list1[:], offs)
-        w4_raw = staged("slot_c", "w4_raw", [P, H], U16)
+        w4_raw = sb("w4_raw", [P, H], U16)
         nc.sync.dma_start(w4_raw[:].bitcast(I32), w4_words[0].bitcast(I32))
-        w4_sc_raw = staged("slot_e", "w4_sc_raw", [P, H], U8)
-        load_scales(nc.vector, nc.gpsimd, w4_sc_raw, w4_scales)
-        tab2_sc = staged("slot_a", "tab2_sc", [P, T], U8)
-        load_scales(nc.vector, nc.scalar, tab2_sc, tab2_scales)
-        tab_sc = staged("slot_b", "tab_sc", [P, T], U8)
-        load_scales(nc.vector, nc.scalar, tab_sc, tab_scales)
         w2_tile(0, 0, "slot_f")
         w2_tile(0, 1, "slot_g")
-        v2_sc1 = sb("v2_sc1", [P, S], U8)
-        nc.vector.memset(v2_sc1[:].bitcast(I32), 0)
+        tab_w = staged("slot_c", "tab_w", [P, T], U32)
+        nc.sync.dma_start(tab_w[:].bitcast(I32), tab_words[0].rearrange("p t i -> p (t i)").bitcast(I32))
+        tab2_sc = staged("slot_a", "tab2_sc", [P, T], U8)
+        load_scales(nc.vector, nc.scalar, tab2_sc, tab2_scales)
+        warm = sb("warm", [P, 2], F32)
+        nc.vector.memset(warm[:, 0:1], 0.0)
+        nc.scalar.activation(warm[:, 1:2], warm[:, 0:1], ABS)
+        tab_sc = staged("slot_b", "tab_sc", [P, T], U8)
+        load_scales(nc.gpsimd, nc.gpsimd, tab_sc, tab_scales)
+        w4_sc_raw = sb("w4_sc_raw", [P, H], U8)
+        load_scales(nc.vector, nc.gpsimd, w4_sc_raw, w4_scales)
 
         w4_w = sb("w4_w", [P, H], U16)
         permute_w4(w4_w, w4_raw)
-        tab_w = staged("slot_c", "tab_w", [P, T], U32)
-        nc.sync.dma_start(tab_w[:].bitcast(I32), tab_words[0].rearrange("p t i -> p (t i)").bitcast(I32))
-
         v2_sc0 = sb("v2_sc0", [P, S], U8)
         nc.vector.tensor_copy(v2_sc0[:], tab2_sc[:].indirect(list2[:]))
-        for q in range(4):
-            nc.gpsimd.dma_start(v2_sc1[32 * q:32 * q + 4, :].bitcast(I32), v2_sc0[32 * q + 4:32 * q + 8, :].bitcast(I32))
-        v2_sc = [v2_sc0, v2_sc1]
         v_sc = sb("v_sc", [P, S], U8)
         nc.vector.tensor_copy(v_sc[:], tab_sc[:].indirect(list1[:]))
         w4_sc = staged("slot_b", "w4_sc", [P, H], U8)
         permute_w4(w4_sc, w4_sc_raw)
-        w8_sc = staged("slot_e", "w8_sc", [P, N], U8)
-        load_scales(nc.vector, nc.sync, w8_sc, w8_scales)
 
         w2_codes, w2_sc = {}, {}
 
-        def quantise_w2(b, a, copy):
-            grouped = sb("w2_bf%d%d" % (b, a), [P, PACK * KP], BF16)
+        def quantise_w2(b, a, copy, slot):
+            grouped = staged(slot, "w2_bf%d%d" % (b, a), [P, PACK * KP], BF16)
             copy(grouped[:].rearrange("p (t m j) -> p m j t", t=PACK, j=PACK),
                  w2_raw[b, a][:].rearrange("p j (m t) -> p m j t", t=PACK))
             w2_codes[b, a] = sb("w2_codes%d%d" % (b, a), [P, KP], U32)
@@ -114,29 +109,37 @@ def tile_list_map_change_gap_kernel(tc, tab_words, tab_scales, tab2_words, tab2_
             nc.vector.tensor_copy(picked[:], window[:].indirect(offsets[:, h * HALF // 16:(h + 1) * HALF // 16]))
             return picked
 
-        quantise_w2(0, 0, nc.scalar.copy)
-        load_tab2(0, "slot_f")
-        quantise_w2(0, 1, nc.scalar.copy)
-        load_tab2(1, "slot_g")
+        load_tab2(0, "slot_a")
+        quantise_w2(0, 0, nc.scalar.copy, "slot_h")
+        load_tab2(1, "slot_f")
+        quantise_w2(0, 1, nc.scalar.copy, "slot_i")
+        v2_sc1 = staged("slot_g", "v2_sc1", [P, S], U8)
+        nc.gpsimd.memset(v2_sc1[:].bitcast(I32), 0)
+        for q in range(4):
+            nc.sync.dma_start(v2_sc1[32 * q:32 * q + 4, :].bitcast(I32), v2_sc0[32 * q + 4:32 * q + 8, :].bitcast(I32))
+        v2_sc = [v2_sc0, v2_sc1]
+
         v_w = [gather_half("v_w%d" % h, U32, tab_w, list1, h) for h in range(2)]
         w2_tile(1, 0, "slot_c")
         v2_w = {(0, h): gather_half("v2_w0%d" % h, U16, tab2_w[0], list2, h) for h in range(2)}
-        w2_tile(1, 1, "slot_f")
+        w2_tile(1, 1, "slot_a")
         for h in range(2):
             v2_w[1, h] = gather_half("v2_w1%d" % h, U16, tab2_w[1], list2, h)
-        load_tw(0, "slot_g")
-        quantise_w2(1, 0, nc.scalar.copy)
+        load_tw(0, "slot_f")
+        quantise_w2(1, 0, nc.scalar.copy, "slot_j")
         w8_w = staged("slot_c", "w8_w", [P, 2 * N], U32)
         nc.sync.dma_start(w8_w[:].bitcast(I32).rearrange("p (b c) -> p b c", b=2),
                           w8_words.rearrange("b p c i -> p b (c i)").bitcast(I32))
-        quantise_w2(1, 1, nc.vector.tensor_copy)
-        load_tw(1, "slot_f")
+        w8_sc = staged("slot_j", "w8_sc", [P, N], U8)
+        load_scales(nc.gpsimd, nc.sync, w8_sc, w8_scales)
+        quantise_w2(1, 1, nc.vector.tensor_copy, "slot_k")
+        load_tw(1, "slot_a")
 
         scan_sb, diff = {}, {}
 
         def scan_chunk(b, c):
             h, col = divmod(c * CH, HALF)
-            acc = psum.tile([P, PACK, CH], F32, name="scan_ps", tag="scan_ps", bufs=2)
+            acc = psum.tile([P, PACK, CH], F32, name="scan_ps", tag="scan_ps", bufs=3)
             for t in range(PACK):
                 cols = slice(KP * b + P * t, KP * b + P * (t + 1))
                 nc.tensor.matmul_mx(out=acc[:, t, :], lhsT=w4_w[:, cols].bitcast(FP4X4), lhsT_scale=w4_sc[:, cols],
@@ -147,7 +150,7 @@ def tile_list_map_change_gap_kernel(tc, tab_words, tab_scales, tab2_words, tab2_
 
         def old_chunk(b, c):
             h, col = divmod(c * CH, HALF)
-            acc = psum.tile([P, PACK, CH], F32, name="old_ps", tag="old_ps", bufs=4)
+            acc = psum.tile([P, PACK, CH], F32, name="old_ps", tag="old_ps", bufs=3)
             for t in range(PACK):
                 cols = slice(P * t, P * (t + 1))
                 for a in range(2):

@@ -63,8 +63,8 @@ def tile_list_map_change_gap_kernel(tc, tab_words, tab_scales, tab2_words, tab2_
                 queue.dma_start(plane[32 * q:32 * q + rows, :].bitcast(I32), scales[:, 4 * q:4 * q + 4, :].bitcast(I32))
 
         def permute_w4(dst, src):
-            nc.vector.tensor_copy(dst[:].rearrange("p (b t m) -> p b m t", b=2, t=PACK),
-                                  src[:].rearrange("p (b m t) -> p b m t", b=2, t=PACK))
+            nc.vector.tensor_copy(dst[:].rearrange("p (b t m) -> p b t m", b=2, t=PACK),
+                                  src[:].rearrange("p (b m t) -> p b t m", b=2, t=PACK))
 
         w2_raw, tab2_w, tw_sb = {}, {}, {}
         nc.sync.dma_start(list2[:], offs2)
@@ -97,9 +97,12 @@ def tile_list_map_change_gap_kernel(tc, tab_words, tab_scales, tab2_words, tab2_
         w2_codes, w2_sc = {}, {}
 
         def quantise_w2(b, a, copy, slot):
+            woven = ring("w2_woven", [P, KP, PACK], BF16, 2)
+            copy(woven[:], w2_raw[b, a][:].rearrange("p j c -> p c j"))
             grouped = staged(slot, "w2_bf%d%d" % (b, a), [P, PACK * KP], BF16)
-            copy(grouped[:].rearrange("p (t m j) -> p m j t", t=PACK, j=PACK),
-                 w2_raw[b, a][:].rearrange("p j (m t) -> p m j t", t=PACK))
+            nc.vector.tensor_copy(
+                grouped[:].bitcast(I32).rearrange("p (t m e) -> p t m e", t=PACK, e=2),
+                woven[:].rearrange("p c j -> p (c j)").bitcast(I32).rearrange("p (m t e) -> p t m e", t=PACK, e=2))
             w2_codes[b, a] = sb("w2_codes%d%d" % (b, a), [P, KP], U32)
             w2_sc[b, a] = sb("w2_sc%d%d" % (b, a), [P, KP], U8)
             nc.vector.quantize_mx(out=w2_codes[b, a][:].bitcast(FP8X4), scales=w2_sc[b, a][:], in_=grouped[:])
@@ -137,37 +140,34 @@ def tile_list_map_change_gap_kernel(tc, tab_words, tab_scales, tab2_words, tab2_
 
         scan_sb, diff = {}, {}
 
-        def scan_chunk(b, c):
-            h, col = divmod(c * CH, HALF)
-            acc = psum.tile([P, PACK, CH], F32, name="scan_ps", tag="scan_ps", bufs=3)
+        def scan_block(b, h):
             for t in range(PACK):
+                acc = psum.tile([P, HALF], F32, name="scan_ps", tag="scan_ps", bufs=3)
                 cols = slice(KP * b + P * t, KP * b + P * (t + 1))
-                nc.tensor.matmul_mx(out=acc[:, t, :], lhsT=w4_w[:, cols].bitcast(FP4X4), lhsT_scale=w4_sc[:, cols],
-                                    rhs=v_w[h][:, col:col + CH].bitcast(FP8X4), rhs_scale=v_sc[:, c * CH:(c + 1) * CH],
+                nc.tensor.matmul_mx(out=acc[:], lhsT=w4_w[:, cols].bitcast(FP4X4), lhsT_scale=w4_sc[:, cols],
+                                    rhs=v_w[h][:].bitcast(FP8X4), rhs_scale=v_sc[:, h * HALF:(h + 1) * HALF],
                                     start=True, stop=True)
-            scan_sb[b, c] = sb("scan%d%d" % (b, c), [P, CH, PACK], F32)
-            nc.scalar.copy(scan_sb[b, c][:], acc[:].rearrange("p t s -> p s t"))
+                scan_sb[b, h, t] = sb("scan%d%d%d" % (b, h, t), [P, HALF], F32)
+                nc.scalar.copy(scan_sb[b, h, t][:], acc[:])
 
-        def old_chunk(b, c):
-            h, col = divmod(c * CH, HALF)
-            acc = psum.tile([P, PACK, CH], F32, name="old_ps", tag="old_ps", bufs=3)
+        def old_block(b, h):
+            diff[b, h] = sb("diff%d%d" % (b, h), [P, PACK, HALF], BF16)
             for t in range(PACK):
+                acc = psum.tile([P, HALF], F32, name="old_ps", tag="old_ps", bufs=3)
                 cols = slice(P * t, P * (t + 1))
                 for a in range(2):
-                    nc.tensor.matmul_mx(out=acc[:, t, :], lhsT=w2_codes[b, a][:, cols].bitcast(FP8X4),
-                                        lhsT_scale=w2_sc[b, a][:, cols],
-                                        rhs=v2_w[a, h][:, col:col + CH].bitcast(FP4X4),
-                                        rhs_scale=v2_sc[a][:, c * CH:(c + 1) * CH], start=(a == 0), stop=(a == 1))
-            diff[b, c] = sb("diff%d%d" % (b, c), [P, CH, PACK], BF16)
-            nc.vector.tensor_tensor(diff[b, c][:], acc[:].rearrange("p t s -> p s t"), scan_sb[b, c][:], ALU.subtract)
+                    nc.tensor.matmul_mx(out=acc[:], lhsT=w2_codes[b, a][:, cols].bitcast(FP8X4),
+                                        lhsT_scale=w2_sc[b, a][:, cols], rhs=v2_w[a, h][:].bitcast(FP4X4),
+                                        rhs_scale=v2_sc[a][:, h * HALF:(h + 1) * HALF], start=(a == 0), stop=(a == 1))
+                nc.vector.tensor_tensor(diff[b, h][:, t, :], acc[:], scan_sb[b, h, t][:], ALU.subtract)
 
         gap_codes, gap_sc = {}, {}
 
         def gap_piece(b, f):
             gap = ring("gap", [P, FIN * PACK], BF16, 4)
-            for i in range(FIN // CH):
-                nc.scalar.activation(gap[:, i * CH * PACK:(i + 1) * CH * PACK],
-                                     diff[b, f * (FIN // CH) + i][:].rearrange("p s t -> p (s t)"), ABS)
+            h, col = divmod(f * FIN, HALF)
+            nc.scalar.activation(gap[:].rearrange("p (s t) -> p s t", t=PACK),
+                                 diff[b, h][:, :, col:col + FIN].rearrange("p t s -> p s t"), ABS)
             gap_codes[b, f] = sb("gap_codes%d%d" % (b, f), [P, FIN], U32)
             gap_sc[b, f] = sb("gap_sc%d%d" % (b, f), [P, FIN], U8)
             nc.vector.quantize_mx(out=gap_codes[b, f][:].bitcast(FP8X4), scales=gap_sc[b, f][:], in_=gap[:])
@@ -188,15 +188,23 @@ def tile_list_map_change_gap_kernel(tc, tab_words, tab_scales, tab2_words, tab2_
                 nc.sync.dma_start(
                     out[2 * P * g:2 * P * (g + 1), FIN * f:FIN * (f + 1)].rearrange("(i p) s -> p i s", p=P), res[:])
 
-        for c in range(NCH):
-            scan_chunk(0, c)
-        for c in range(NCH):
-            old_chunk(0, c)
-        for c in range(NCH):
-            scan_chunk(1, c)
-        for f in range(S // FIN):
-            for i in range(FIN // CH):
-                old_chunk(1, f * (FIN // CH) + i)
-            gap_piece(0, f)
-            gap_piece(1, f)
-            final_piece(f)
+        scan_block(0, 0)
+        scan_block(0, 1)
+        old_block(0, 0)
+        old_block(0, 1)
+        scan_block(1, 0)
+        scan_block(1, 1)
+        gap_piece(0, 0)
+        gap_piece(0, 1)
+        gap_piece(0, 2)
+        old_block(1, 0)
+        old_block(1, 1)
+        gap_piece(1, 0)
+        final_piece(0)
+        gap_piece(1, 1)
+        final_piece(1)
+        gap_piece(0, 3)
+        gap_piece(1, 2)
+        final_piece(2)
+        gap_piece(1, 3)
+        final_piece(3)

@@ -67,42 +67,47 @@ def tile_list_map_change_gap_kernel(tc, tab_words, tab_scales, tab2_words, tab2_
                                   src[:].rearrange("p (b m t) -> p b t m", b=2, t=PACK))
 
         w2_raw, tab2_w, tw_sb = {}, {}, {}
+        w4_raw = staged("slot_c", "w4_raw", [P, H], U16)
+        nc.sync.dma_start(w4_raw[:].bitcast(I32), w4_words[0].bitcast(I32))
         nc.sync.dma_start(list2[:], offs2)
         nc.sync.dma_start(list1[:], offs)
-        w4_raw = sb("w4_raw", [P, H], U16)
-        nc.sync.dma_start(w4_raw[:].bitcast(I32), w4_words[0].bitcast(I32))
-        w2_tile(0, 0, "slot_f")
-        w2_tile(0, 1, "slot_g")
-        tab_w = staged("slot_c", "tab_w", [P, T], U32)
-        nc.sync.dma_start(tab_w[:].bitcast(I32), tab_words[0].rearrange("p t i -> p (t i)").bitcast(I32))
         tab2_sc = staged("slot_a", "tab2_sc", [P, T], U8)
-        load_scales(nc.vector, nc.scalar, tab2_sc, tab2_scales)
-        warm = sb("warm", [P, 2], F32)
-        nc.vector.memset(warm[:, 0:1], 0.0)
-        nc.scalar.activation(warm[:, 1:2], warm[:, 0:1], ABS)
+        load_scales(nc.vector, nc.sync, tab2_sc, tab2_scales)
         tab_sc = staged("slot_b", "tab_sc", [P, T], U8)
-        load_scales(nc.gpsimd, nc.gpsimd, tab_sc, tab_scales)
+        load_scales(nc.vector, nc.sync, tab_sc, tab_scales)
         w4_sc_raw = sb("w4_sc_raw", [P, H], U8)
-        load_scales(nc.vector, nc.gpsimd, w4_sc_raw, w4_scales)
+        load_scales(nc.vector, nc.sync, w4_sc_raw, w4_scales)
+        warm = sb("warm", [P, 2], F32)
+        nc.gpsimd.memset(warm[:, 0:1], 0.0)
+        nc.scalar.activation(warm[:, 1:2], warm[:, 0:1], ABS)
+        v2_sc1 = sb("v2_sc1", [P, S], U8)
+        nc.gpsimd.memset(v2_sc1[:].bitcast(I32), 0)
 
         w4_w = sb("w4_w", [P, H], U16)
         permute_w4(w4_w, w4_raw)
+        tab_w = staged("slot_c", "tab_w", [P, T], U32)
+        for u in range(2):
+            cols = slice(u * T // 2, (u + 1) * T // 2)
+            nc.sync.dma_start(tab_w[:, cols].bitcast(I32),
+                              tab_words[0][:, cols, :].rearrange("p t i -> p (t i)").bitcast(I32))
         v2_sc0 = sb("v2_sc0", [P, S], U8)
         nc.vector.tensor_copy(v2_sc0[:], tab2_sc[:].indirect(list2[:]))
+        w2_tile(0, 0, "slot_a")
+        for q in range(4):
+            nc.sync.dma_start(v2_sc1[32 * q:32 * q + 4, :].bitcast(I32), v2_sc0[32 * q + 4:32 * q + 8, :].bitcast(I32))
+        v2_sc = [v2_sc0, v2_sc1]
         v_sc = sb("v_sc", [P, S], U8)
         nc.vector.tensor_copy(v_sc[:], tab_sc[:].indirect(list1[:]))
-        w4_sc = staged("slot_b", "w4_sc", [P, H], U8)
+        w2_tile(0, 1, "slot_b")
+        w4_sc = sb("w4_sc", [P, H], U8)
         permute_w4(w4_sc, w4_sc_raw)
 
         w2_codes, w2_sc = {}, {}
 
         def quantise_w2(b, a, copy, slot):
-            woven = ring("w2_woven", [P, KP, PACK], BF16, 2)
-            copy(woven[:], w2_raw[b, a][:].rearrange("p j c -> p c j"))
             grouped = staged(slot, "w2_bf%d%d" % (b, a), [P, PACK * KP], BF16)
-            nc.vector.tensor_copy(
-                grouped[:].bitcast(I32).rearrange("p (t m e) -> p t m e", t=PACK, e=2),
-                woven[:].rearrange("p c j -> p (c j)").bitcast(I32).rearrange("p (m t e) -> p t m e", t=PACK, e=2))
+            copy(grouped[:].rearrange("p (t m j) -> p m j t", t=PACK, j=PACK),
+                 w2_raw[b, a][:].rearrange("p j (m t) -> p m j t", t=PACK))
             w2_codes[b, a] = sb("w2_codes%d%d" % (b, a), [P, KP], U32)
             w2_sc[b, a] = sb("w2_sc%d%d" % (b, a), [P, KP], U8)
             nc.vector.quantize_mx(out=w2_codes[b, a][:].bitcast(FP8X4), scales=w2_sc[b, a][:], in_=grouped[:])
@@ -112,37 +117,31 @@ def tile_list_map_change_gap_kernel(tc, tab_words, tab_scales, tab2_words, tab2_
             nc.vector.tensor_copy(picked[:], window[:].indirect(offsets[:, h * HALF // 16:(h + 1) * HALF // 16]))
             return picked
 
-        load_tab2(0, "slot_a")
-        quantise_w2(0, 0, nc.scalar.copy, "slot_h")
-        load_tab2(1, "slot_f")
-        quantise_w2(0, 1, nc.scalar.copy, "slot_i")
-        v2_sc1 = staged("slot_g", "v2_sc1", [P, S], U8)
-        nc.gpsimd.memset(v2_sc1[:].bitcast(I32), 0)
-        for q in range(4):
-            nc.sync.dma_start(v2_sc1[32 * q:32 * q + 4, :].bitcast(I32), v2_sc0[32 * q + 4:32 * q + 8, :].bitcast(I32))
-        v2_sc = [v2_sc0, v2_sc1]
-
         v_w = [gather_half("v_w%d" % h, U32, tab_w, list1, h) for h in range(2)]
-        w2_tile(1, 0, "slot_c")
+        load_tab2(0, "slot_c")
+        quantise_w2(0, 0, nc.vector.tensor_copy, "slot_h")
+        load_tab2(1, "slot_a")
+        quantise_w2(0, 1, nc.vector.tensor_copy, "slot_i")
+        w2_tile(1, 0, "slot_b")
         v2_w = {(0, h): gather_half("v2_w0%d" % h, U16, tab2_w[0], list2, h) for h in range(2)}
-        w2_tile(1, 1, "slot_a")
+        w2_tile(1, 1, "slot_c")
         for h in range(2):
             v2_w[1, h] = gather_half("v2_w1%d" % h, U16, tab2_w[1], list2, h)
-        load_tw(0, "slot_f")
+        load_tw(0, "slot_a")
         quantise_w2(1, 0, nc.scalar.copy, "slot_j")
-        w8_w = staged("slot_c", "w8_w", [P, 2 * N], U32)
+        w8_w = staged("slot_b", "w8_w", [P, 2 * N], U32)
         nc.sync.dma_start(w8_w[:].bitcast(I32).rearrange("p (b c) -> p b c", b=2),
                           w8_words.rearrange("b p c i -> p b (c i)").bitcast(I32))
         w8_sc = staged("slot_j", "w8_sc", [P, N], U8)
         load_scales(nc.gpsimd, nc.sync, w8_sc, w8_scales)
-        quantise_w2(1, 1, nc.vector.tensor_copy, "slot_k")
-        load_tw(1, "slot_a")
+        quantise_w2(1, 1, nc.scalar.copy, "slot_k")
+        load_tw(1, "slot_c")
 
         scan_sb, diff = {}, {}
 
         def scan_block(b, h):
             for t in range(PACK):
-                acc = psum.tile([P, HALF], F32, name="scan_ps", tag="scan_ps", bufs=3)
+                acc = psum.tile([P, HALF], F32, name="scan_ps", tag="y_ps", bufs=4)
                 cols = slice(KP * b + P * t, KP * b + P * (t + 1))
                 nc.tensor.matmul_mx(out=acc[:], lhsT=w4_w[:, cols].bitcast(FP4X4), lhsT_scale=w4_sc[:, cols],
                                     rhs=v_w[h][:].bitcast(FP8X4), rhs_scale=v_sc[:, h * HALF:(h + 1) * HALF],
@@ -153,7 +152,7 @@ def tile_list_map_change_gap_kernel(tc, tab_words, tab_scales, tab2_words, tab2_
         def old_block(b, h):
             diff[b, h] = sb("diff%d%d" % (b, h), [P, PACK, HALF], BF16)
             for t in range(PACK):
-                acc = psum.tile([P, HALF], F32, name="old_ps", tag="old_ps", bufs=3)
+                acc = psum.tile([P, HALF], F32, name="old_ps", tag="old_ps", bufs=4)
                 cols = slice(P * t, P * (t + 1))
                 for a in range(2):
                     nc.tensor.matmul_mx(out=acc[:], lhsT=w2_codes[b, a][:, cols].bitcast(FP8X4),
@@ -166,15 +165,15 @@ def tile_list_map_change_gap_kernel(tc, tab_words, tab_scales, tab2_words, tab2_
         def gap_piece(b, f):
             gap = ring("gap", [P, FIN * PACK], BF16, 4)
             h, col = divmod(f * FIN, HALF)
-            nc.scalar.activation(gap[:].rearrange("p (s t) -> p s t", t=PACK),
-                                 diff[b, h][:, :, col:col + FIN].rearrange("p t s -> p s t"), ABS)
+            nc.scalar.activation(gap[:].rearrange("p (c i t) -> p c t i", i=4, t=PACK),
+                                 diff[b, h][:, :, col:col + FIN].rearrange("p t (c i) -> p c t i", i=4), ABS)
             gap_codes[b, f] = sb("gap_codes%d%d" % (b, f), [P, FIN], U32)
             gap_sc[b, f] = sb("gap_sc%d%d" % (b, f), [P, FIN], U8)
             nc.vector.quantize_mx(out=gap_codes[b, f][:].bitcast(FP8X4), scales=gap_sc[b, f][:], in_=gap[:])
 
         def final_piece(f):
             for g in range(2):
-                acc = psum.tile([P, 2, FIN], F32, name="y_ps", tag="y_ps", bufs=2)
+                acc = psum.tile([P, 2, FIN], F32, name="y_ps", tag="y_ps", bufs=4)
                 for i in range(2):
                     cols = slice(P * (2 * g + i), P * (2 * g + i + 1))
                     for b in range(2):
@@ -188,23 +187,16 @@ def tile_list_map_change_gap_kernel(tc, tab_words, tab_scales, tab2_words, tab2_
                 nc.sync.dma_start(
                     out[2 * P * g:2 * P * (g + 1), FIN * f:FIN * (f + 1)].rearrange("(i p) s -> p i s", p=P), res[:])
 
-        scan_block(0, 0)
-        scan_block(0, 1)
-        old_block(0, 0)
-        old_block(0, 1)
-        scan_block(1, 0)
-        scan_block(1, 1)
-        gap_piece(0, 0)
-        gap_piece(0, 1)
-        gap_piece(0, 2)
-        old_block(1, 0)
-        old_block(1, 1)
-        gap_piece(1, 0)
-        final_piece(0)
-        gap_piece(1, 1)
-        final_piece(1)
-        gap_piece(0, 3)
-        gap_piece(1, 2)
-        final_piece(2)
-        gap_piece(1, 3)
-        final_piece(3)
+        for h in range(2):
+            scan_block(0, h)
+        for h in range(2):
+            old_block(0, h)
+        for h in range(2):
+            scan_block(1, h)
+        for h in range(2):
+            old_block(1, h)
+        for f in range(S // FIN):
+            gap_piece(0, f)
+            gap_piece(1, f)
+        for f in range(S // FIN):
+            final_piece(f)

@@ -18,11 +18,12 @@ ABS = mybir.ActivationFunctionType.Abs
 
 P = 128
 PACK = 4
-KP = P * PACK
+PASS = P * PACK
+QUADRANTS = 4
 HALF = S // 2
-CH = 128
-NCH = S // CH
-FIN = 256
+PIECE = 256
+RUN = 4
+BANKS = 4
 
 
 def tile_list_map_change_gap_kernel(tc, tab_words, tab_scales, tab2_words, tab2_scales, offs, offs2,
@@ -32,127 +33,126 @@ def tile_list_map_change_gap_kernel(tc, tab_words, tab_scales, tab2_words, tab2_
         keep = ctx.enter_context(tc.tile_pool(name="keep", bufs=1))
         psum = ctx.enter_context(tc.psum_pool(name="psum", bufs=1))
 
-        def sb(name, shape, dtype):
+        def own(name, shape, dtype):
             return keep.tile(shape, dtype, name=name, align_bytes=64)
 
-        def ring(name, shape, dtype, bufs):
-            return keep.tile(shape, dtype, name=name, tag=name, bufs=bufs, align_bytes=64)
+        def staged(area, name, shape, dtype):
+            return keep.tile(shape, dtype, name=name, tag=area, bufs=1, align_bytes=64)
 
         list1 = keep.tile([P, S // 16], U16, name="list1")
         list2 = keep.tile([P, S // 16], U16, name="list2")
-        def staged(slot, name, shape, dtype):
-            return keep.tile(shape, dtype, name=name, tag=slot, bufs=1, align_bytes=64)
+        w2_raw, tab2_w, tw_sb = {}, {}, {}
 
-        def w2_tile(b, a, slot):
-            w2_raw[b, a] = staged(slot, "w2_raw%d%d" % (b, a), [P, PACK, KP], F32)
-            nc.sync.dma_start(w2_raw[b, a][:],
-                              w2[KP * a:KP * (a + 1), KP * b:KP * (b + 1)].rearrange("(p j) c -> p j c", j=PACK))
+        def load_w2(b, a, area):
+            w2_raw[b, a] = staged(area, "w2_raw%d%d" % (b, a), [P, PACK, PASS], F32)
+            nc.sync.dma_start(
+                w2_raw[b, a][:],
+                w2[PASS * a:PASS * (a + 1), PASS * b:PASS * (b + 1)].rearrange("(p j) c -> p j c", j=PACK))
 
-        def load_tab2(a, slot):
-            tab2_w[a] = staged(slot, "tab2_w%d" % a, [P, T], U16)
+        def load_tab2(a, area):
+            tab2_w[a] = staged(area, "tab2_w%d" % a, [P, T], U16)
             nc.sync.dma_start(tab2_w[a][:].bitcast(I32), tab2_words[a].bitcast(I32))
 
-        def load_tw(u, slot):
-            tw_sb[u] = staged(slot, "tw%d" % u, [P, N // P, HALF], F32)
-            nc.sync.dma_start(tw_sb[u][:], tw[:, HALF * u:HALF * (u + 1)].rearrange("(nt p) s -> p nt s", p=P))
+        def load_tw(h, area):
+            tw_sb[h] = staged(area, "tw%d" % h, [P, N // P, HALF], F32)
+            nc.sync.dma_start(tw_sb[h][:], tw[:, HALF * h:HALF * (h + 1)].rearrange("(nt p) s -> p nt s", p=P))
 
-        def load_scales(clear, queue, plane, scales):
+        def load_scales(clearing_engine, plane, scales):
             rows = 4 * scales.shape[0]
-            clear.memset(plane[:].bitcast(I32), 0)
-            for q in range(4):
-                queue.dma_start(plane[32 * q:32 * q + rows, :].bitcast(I32), scales[:, 4 * q:4 * q + 4, :].bitcast(I32))
+            clearing_engine.memset(plane[:].bitcast(I32), 0)
+            for q in range(QUADRANTS):
+                nc.sync.dma_start(plane[32 * q:32 * q + rows, :].bitcast(I32),
+                                  scales[:, 4 * q:4 * q + 4, :].bitcast(I32))
 
-        def permute_w4(dst, src):
+        def reorder_w4(dst, src):
             nc.vector.tensor_copy(dst[:].rearrange("p (b t m) -> p b t m", b=2, t=PACK),
                                   src[:].rearrange("p (b m t) -> p b t m", b=2, t=PACK))
 
-        w2_raw, tab2_w, tw_sb = {}, {}, {}
-        w4_raw = staged("slot_c", "w4_raw", [P, H], U16)
+        w4_raw = staged("area_c", "w4_raw", [P, H], U16)
         nc.sync.dma_start(w4_raw[:].bitcast(I32), w4_words[0].bitcast(I32))
         nc.sync.dma_start(list2[:], offs2)
         nc.sync.dma_start(list1[:], offs)
-        tab2_sc = staged("slot_a", "tab2_sc", [P, T], U8)
-        load_scales(nc.vector, nc.sync, tab2_sc, tab2_scales)
-        tab_sc = staged("slot_b", "tab_sc", [P, T], U8)
-        load_scales(nc.vector, nc.sync, tab_sc, tab_scales)
-        w4_sc_raw = sb("w4_sc_raw", [P, H], U8)
-        load_scales(nc.vector, nc.sync, w4_sc_raw, w4_scales)
-        warm = sb("warm", [P, 2], F32)
-        nc.gpsimd.memset(warm[:, 0:1], 0.0)
-        nc.scalar.activation(warm[:, 1:2], warm[:, 0:1], ABS)
-        v2_sc1 = sb("v2_sc1", [P, S], U8)
+        tab2_sc = staged("area_a", "tab2_sc", [P, T], U8)
+        load_scales(nc.vector, tab2_sc, tab2_scales)
+        tab_sc = staged("area_b", "tab_sc", [P, T], U8)
+        load_scales(nc.vector, tab_sc, tab_scales)
+        w4_sc_raw = own("w4_sc_raw", [P, H], U8)
+        load_scales(nc.vector, w4_sc_raw, w4_scales)
+        v2_sc1 = own("v2_sc1", [P, S], U8)
         nc.gpsimd.memset(v2_sc1[:].bitcast(I32), 0)
 
-        w4_w = sb("w4_w", [P, H], U16)
-        permute_w4(w4_w, w4_raw)
-        tab_w = staged("slot_c", "tab_w", [P, T], U32)
+        w4_w = own("w4_w", [P, H], U16)
+        reorder_w4(w4_w, w4_raw)
+        tab_w = staged("area_c", "tab_w", [P, T], U32)
         for u in range(2):
             cols = slice(u * T // 2, (u + 1) * T // 2)
             nc.sync.dma_start(tab_w[:, cols].bitcast(I32),
                               tab_words[0][:, cols, :].rearrange("p t i -> p (t i)").bitcast(I32))
-        v2_sc0 = sb("v2_sc0", [P, S], U8)
+
+        v2_sc0 = own("v2_sc0", [P, S], U8)
         nc.vector.tensor_copy(v2_sc0[:], tab2_sc[:].indirect(list2[:]))
-        w2_tile(0, 0, "slot_a")
-        for q in range(4):
-            nc.sync.dma_start(v2_sc1[32 * q:32 * q + 4, :].bitcast(I32), v2_sc0[32 * q + 4:32 * q + 8, :].bitcast(I32))
+        load_w2(0, 0, "area_a")
+        for q in range(QUADRANTS):
+            nc.sync.dma_start(v2_sc1[32 * q:32 * q + 4, :].bitcast(I32),
+                              v2_sc0[32 * q + 4:32 * q + 8, :].bitcast(I32))
         v2_sc = [v2_sc0, v2_sc1]
-        v_sc = sb("v_sc", [P, S], U8)
+        v_sc = own("v_sc", [P, S], U8)
         nc.vector.tensor_copy(v_sc[:], tab_sc[:].indirect(list1[:]))
-        w2_tile(0, 1, "slot_b")
-        w4_sc = sb("w4_sc", [P, H], U8)
-        permute_w4(w4_sc, w4_sc_raw)
+        load_w2(0, 1, "area_b")
+        w4_sc = own("w4_sc", [P, H], U8)
+        reorder_w4(w4_sc, w4_sc_raw)
 
         w2_codes, w2_sc = {}, {}
 
-        def quantise_w2(b, a, copy, slot):
-            grouped = staged(slot, "w2_bf%d%d" % (b, a), [P, PACK * KP], BF16)
-            copy(grouped[:].rearrange("p (t m j) -> p m j t", t=PACK, j=PACK),
+        def quantise_w2(b, a, cast):
+            grouped = staged("w2_bf%d%d" % (b, a), "w2_bf%d%d" % (b, a), [P, PACK * PASS], BF16)
+            cast(grouped[:].rearrange("p (t m j) -> p m j t", t=PACK, j=PACK),
                  w2_raw[b, a][:].rearrange("p j (m t) -> p m j t", t=PACK))
-            w2_codes[b, a] = sb("w2_codes%d%d" % (b, a), [P, KP], U32)
-            w2_sc[b, a] = sb("w2_sc%d%d" % (b, a), [P, KP], U8)
+            w2_codes[b, a] = own("w2_codes%d%d" % (b, a), [P, PASS], U32)
+            w2_sc[b, a] = own("w2_sc%d%d" % (b, a), [P, PASS], U8)
             nc.vector.quantize_mx(out=w2_codes[b, a][:].bitcast(FP8X4), scales=w2_sc[b, a][:], in_=grouped[:])
 
         def gather_half(name, dtype, window, offsets, h):
-            picked = sb(name, [P, HALF], dtype)
+            picked = own(name, [P, HALF], dtype)
             nc.vector.tensor_copy(picked[:], window[:].indirect(offsets[:, h * HALF // 16:(h + 1) * HALF // 16]))
             return picked
 
         v_w = [gather_half("v_w%d" % h, U32, tab_w, list1, h) for h in range(2)]
-        load_tab2(0, "slot_c")
-        quantise_w2(0, 0, nc.vector.tensor_copy, "slot_h")
-        load_tab2(1, "slot_a")
-        quantise_w2(0, 1, nc.vector.tensor_copy, "slot_i")
-        w2_tile(1, 0, "slot_b")
+        load_tab2(0, "area_c")
+        quantise_w2(0, 0, nc.vector.tensor_copy)
+        load_tab2(1, "area_a")
+        quantise_w2(0, 1, nc.vector.tensor_copy)
+        load_w2(1, 0, "area_b")
         v2_w = {(0, h): gather_half("v2_w0%d" % h, U16, tab2_w[0], list2, h) for h in range(2)}
-        w2_tile(1, 1, "slot_c")
+        load_w2(1, 1, "area_c")
         for h in range(2):
             v2_w[1, h] = gather_half("v2_w1%d" % h, U16, tab2_w[1], list2, h)
-        load_tw(0, "slot_a")
-        quantise_w2(1, 0, nc.scalar.copy, "slot_j")
-        w8_w = staged("slot_b", "w8_w", [P, 2 * N], U32)
+        load_tw(0, "area_a")
+        quantise_w2(1, 0, nc.scalar.copy)
+        w8_w = staged("area_b", "w8_w", [P, 2 * N], U32)
         nc.sync.dma_start(w8_w[:].bitcast(I32).rearrange("p (b c) -> p b c", b=2),
                           w8_words.rearrange("b p c i -> p b (c i)").bitcast(I32))
-        w8_sc = staged("slot_j", "w8_sc", [P, N], U8)
-        load_scales(nc.gpsimd, nc.sync, w8_sc, w8_scales)
-        quantise_w2(1, 1, nc.scalar.copy, "slot_k")
-        load_tw(1, "slot_c")
+        w8_sc = staged("w2_bf10", "w8_sc", [P, N], U8)
+        load_scales(nc.gpsimd, w8_sc, w8_scales)
+        quantise_w2(1, 1, nc.scalar.copy)
+        load_tw(1, "area_c")
 
-        scan_sb, diff = {}, {}
+        scan_sb, diff, gap_codes, gap_sc = {}, {}, {}, {}
 
         def scan_block(b, h):
             for t in range(PACK):
-                acc = psum.tile([P, HALF], F32, name="scan_ps", tag="y_ps", bufs=4)
-                cols = slice(KP * b + P * t, KP * b + P * (t + 1))
+                acc = psum.tile([P, HALF], F32, name="scan_ps", tag="scan_then_y", bufs=BANKS)
+                cols = slice(PASS * b + P * t, PASS * b + P * (t + 1))
                 nc.tensor.matmul_mx(out=acc[:], lhsT=w4_w[:, cols].bitcast(FP4X4), lhsT_scale=w4_sc[:, cols],
                                     rhs=v_w[h][:].bitcast(FP8X4), rhs_scale=v_sc[:, h * HALF:(h + 1) * HALF],
                                     start=True, stop=True)
-                scan_sb[b, h, t] = sb("scan%d%d%d" % (b, h, t), [P, HALF], F32)
+                scan_sb[b, h, t] = own("scan%d%d%d" % (b, h, t), [P, HALF], F32)
                 nc.scalar.copy(scan_sb[b, h, t][:], acc[:])
 
         def old_block(b, h):
-            diff[b, h] = sb("diff%d%d" % (b, h), [P, PACK, HALF], BF16)
+            diff[b, h] = own("diff%d%d" % (b, h), [P, PACK, HALF], BF16)
             for t in range(PACK):
-                acc = psum.tile([P, HALF], F32, name="old_ps", tag="old_ps", bufs=4)
+                acc = psum.tile([P, HALF], F32, name="old_ps", tag="old", bufs=BANKS)
                 cols = slice(P * t, P * (t + 1))
                 for a in range(2):
                     nc.tensor.matmul_mx(out=acc[:], lhsT=w2_codes[b, a][:, cols].bitcast(FP8X4),
@@ -160,43 +160,42 @@ def tile_list_map_change_gap_kernel(tc, tab_words, tab_scales, tab2_words, tab2_
                                         rhs_scale=v2_sc[a][:, h * HALF:(h + 1) * HALF], start=(a == 0), stop=(a == 1))
                 nc.vector.tensor_tensor(diff[b, h][:, t, :], acc[:], scan_sb[b, h, t][:], ALU.subtract)
 
-        gap_codes, gap_sc = {}, {}
-
         def gap_piece(b, f):
-            gap = ring("gap", [P, FIN * PACK], BF16, 4)
-            h, col = divmod(f * FIN, HALF)
-            nc.scalar.activation(gap[:].rearrange("p (c i t) -> p c t i", i=4, t=PACK),
-                                 diff[b, h][:, :, col:col + FIN].rearrange("p t (c i) -> p c t i", i=4), ABS)
-            gap_codes[b, f] = sb("gap_codes%d%d" % (b, f), [P, FIN], U32)
-            gap_sc[b, f] = sb("gap_sc%d%d" % (b, f), [P, FIN], U8)
+            gap = own("gap%d%d" % (b, f), [P, PIECE * PACK], BF16)
+            h, col = divmod(f * PIECE, HALF)
+            nc.scalar.activation(gap[:].rearrange("p (c i t) -> p c t i", i=RUN, t=PACK),
+                                 diff[b, h][:, :, col:col + PIECE].rearrange("p t (c i) -> p c t i", i=RUN), ABS)
+            gap_codes[b, f] = own("gap_codes%d%d" % (b, f), [P, PIECE], U32)
+            gap_sc[b, f] = own("gap_sc%d%d" % (b, f), [P, PIECE], U8)
             nc.vector.quantize_mx(out=gap_codes[b, f][:].bitcast(FP8X4), scales=gap_sc[b, f][:], in_=gap[:])
 
         def final_piece(f):
+            h, col = divmod(f * PIECE, HALF)
             for g in range(2):
-                acc = psum.tile([P, 2, FIN], F32, name="y_ps", tag="y_ps", bufs=4)
+                acc = psum.tile([P, 2, PIECE], F32, name="y_ps", tag="scan_then_y", bufs=BANKS)
                 for i in range(2):
-                    cols = slice(P * (2 * g + i), P * (2 * g + i + 1))
+                    first = P * (2 * g + i)
                     for b in range(2):
-                        nc.tensor.matmul_mx(out=acc[:, i, :], lhsT=w8_w[:, N * b + cols.start:N * b + cols.stop].bitcast(FP8X4),
-                                            lhsT_scale=w8_sc[4 * b:P, cols], rhs=gap_codes[b, f][:].bitcast(FP8X4),
-                                            rhs_scale=gap_sc[b, f][:], start=(b == 0), stop=(b == 1))
-                weighted = ring("weighted", [P, 2, FIN], F32, 3)
-                nc.vector.tensor_tensor(weighted[:], acc[:], tw_sb[f // 2][:, 2 * g:2 * g + 2, FIN * (f % 2):FIN * (f % 2 + 1)], ALU.mult)
-                res = ring("res", [P, 2, FIN], F32, 4)
+                        nc.tensor.matmul_mx(out=acc[:, i, :],
+                                            lhsT=w8_w[:, N * b + first:N * b + first + P].bitcast(FP8X4),
+                                            lhsT_scale=w8_sc[4 * b:P, first:first + P],
+                                            rhs=gap_codes[b, f][:].bitcast(FP8X4), rhs_scale=gap_sc[b, f][:],
+                                            start=(b == 0), stop=(b == 1))
+                weighted = own("weighted%d%d" % (f, g), [P, 2, PIECE], F32)
+                nc.vector.tensor_tensor(weighted[:], acc[:], tw_sb[h][:, 2 * g:2 * g + 2, col:col + PIECE], ALU.mult)
+                res = own("res%d%d" % (f, g), [P, 2, PIECE], F32)
                 nc.scalar.activation(res[:], weighted[:], ABS)
                 nc.sync.dma_start(
-                    out[2 * P * g:2 * P * (g + 1), FIN * f:FIN * (f + 1)].rearrange("(i p) s -> p i s", p=P), res[:])
+                    out[2 * P * g:2 * P * (g + 1), PIECE * f:PIECE * (f + 1)].rearrange("(i p) s -> p i s", p=P),
+                    res[:])
 
-        for h in range(2):
-            scan_block(0, h)
-        for h in range(2):
-            old_block(0, h)
-        for h in range(2):
-            scan_block(1, h)
-        for h in range(2):
-            old_block(1, h)
-        for f in range(S // FIN):
-            gap_piece(0, f)
-            gap_piece(1, f)
-        for f in range(S // FIN):
+        for b in range(2):
+            for h in range(2):
+                scan_block(b, h)
+            for h in range(2):
+                old_block(b, h)
+        for f in range(S // PIECE):
+            for b in range(2):
+                gap_piece(b, f)
+        for f in range(S // PIECE):
             final_piece(f)

@@ -20,10 +20,12 @@ P = 128
 PACK = 4
 PASS = P * PACK
 QUADRANTS = 4
+ROWS = 16
 HALF = S // 2
 PIECE = 256
 RUN = 4
-BANKS = 4
+BANKS = 8
+KB = 1024
 
 
 def tile_list_map_change_gap_kernel(tc, tab_words, tab_scales, tab2_words, tab2_scales, offs, offs2,
@@ -31,133 +33,154 @@ def tile_list_map_change_gap_kernel(tc, tab_words, tab_scales, tab2_words, tab2_
     nc = tc.nc
     with ExitStack() as ctx:
         keep = ctx.enter_context(tc.tile_pool(name="keep", bufs=1))
+        shared = ctx.enter_context(tc.tile_pool(name="shared", bufs=1))
         psum = ctx.enter_context(tc.psum_pool(name="psum", bufs=1))
 
         def own(name, shape, dtype):
             return keep.tile(shape, dtype, name=name, align_bytes=64)
 
-        def staged(area, name, shape, dtype):
-            return keep.tile(shape, dtype, name=name, tag=area, bufs=1, align_bytes=64)
+        def placed(offset, name, shape, dtype):
+            return shared.tile(shape, dtype, name=name, align_bytes=64, offset=offset)
+
+        area_a, area_b, area_c, area_d, area_e = 0, 16 * KB, 32 * KB, 40 * KB, 44 * KB
 
         list1 = keep.tile([P, S // 16], U16, name="list1")
         list2 = keep.tile([P, S // 16], U16, name="list2")
         w2_raw, tab2_w, tw_sb = {}, {}, {}
 
-        def load_w2(b, a, area):
-            w2_raw[b, a] = staged(area, "w2_raw%d%d" % (b, a), [P, PACK, PASS], F32)
+        def load_w2(b, a, tile):
+            w2_raw[b, a] = tile
             nc.sync.dma_start(
-                w2_raw[b, a][:],
-                w2[PASS * a:PASS * (a + 1), PASS * b:PASS * (b + 1)].rearrange("(p j) c -> p j c", j=PACK))
+                tile[:], w2[PASS * a:PASS * (a + 1), PASS * b:PASS * (b + 1)].rearrange("(p j) c -> p j c", j=PACK))
 
-        def load_tab2(a, area):
-            tab2_w[a] = staged(area, "tab2_w%d" % a, [P, T], U16)
+        def load_tab2(a):
+            tab2_w[a] = placed(area_a + 8 * KB * a, "tab2_w%d" % a, [P, T], U16)
             nc.sync.dma_start(tab2_w[a][:].bitcast(I32), tab2_words[a].bitcast(I32))
 
-        def load_tw(h, area):
-            tw_sb[h] = staged(area, "tw%d" % h, [P, N // P, HALF], F32)
+        def load_tw(h):
+            tw_sb[h] = placed(area_a + 8 * KB * h, "tw%d" % h, [P, N // P, HALF], F32)
             nc.sync.dma_start(tw_sb[h][:], tw[:, HALF * h:HALF * (h + 1)].rearrange("(nt p) s -> p nt s", p=P))
 
-        def load_scales(clearing_engine, plane, scales):
-            rows = 4 * scales.shape[0]
-            clearing_engine.memset(plane[:].bitcast(I32), 0)
+        def load_rows(tile, scales, clearing_engine):
+            rows = scales.rearrange("a q c -> (a q) c")
+            first = P - rows.shape[0]
+            nc.sync.dma_start(tile[first:P, :].bitcast(I32), rows.bitcast(I32))
+            clearing_engine.memset(tile[0:first, :].bitcast(I32), 0)
+
+        def move_rows(plane, rows, first):
             for q in range(QUADRANTS):
-                nc.sync.dma_start(plane[32 * q:32 * q + rows, :].bitcast(I32),
-                                  scales[:, 4 * q:4 * q + 4, :].bitcast(I32))
+                nc.sync.dma_start(plane[32 * q:32 * q + 4, :].bitcast(I32),
+                                  rows[first + 4 * q:first + 4 * q + 4, :].bitcast(I32))
 
         def reorder_w4(dst, src):
-            nc.vector.tensor_copy(dst[:].rearrange("p (b t m) -> p b t m", b=2, t=PACK),
-                                  src[:].rearrange("p (b m t) -> p b t m", b=2, t=PACK))
+            nc.vector.tensor_copy(dst.rearrange("p (b t m) -> p b t m", b=2, t=PACK),
+                                  src.rearrange("p (b m t) -> p b t m", b=2, t=PACK))
 
-        w4_raw = staged("area_c", "w4_raw", [P, H], U16)
+        w4_rows = own("w4_rows", [P, H], U8)
+        load_rows(w4_rows, w4_scales, nc.vector)
+        w4_raw = own("w4_raw", [P, H], U16)
         nc.sync.dma_start(w4_raw[:].bitcast(I32), w4_words[0].bitcast(I32))
-        nc.sync.dma_start(list2[:], offs2)
         nc.sync.dma_start(list1[:], offs)
-        tab2_sc = staged("area_a", "tab2_sc", [P, T], U8)
-        load_scales(nc.vector, tab2_sc, tab2_scales)
-        tab_sc = staged("area_b", "tab_sc", [P, T], U8)
-        load_scales(nc.vector, tab_sc, tab_scales)
-        w4_sc_raw = own("w4_sc_raw", [P, H], U8)
-        load_scales(nc.vector, w4_sc_raw, w4_scales)
-        v2_sc1 = own("v2_sc1", [P, S], U8)
-        nc.gpsimd.memset(v2_sc1[:].bitcast(I32), 0)
+        tab_rows = own("tab_rows", [P, T], U8)
+        load_rows(tab_rows, tab_scales, nc.vector)
+        nc.sync.dma_start(list2[:], offs2)
+        tab2_rows = placed(area_c, "tab2_rows", [P, T], U8)
+        load_rows(tab2_rows, tab2_scales, nc.gpsimd)
+        load_w2(0, 0, own("w2_raw00", [P, PACK, PASS], F32))
+        tab_w = placed(area_b, "tab_w", [P, T], U32)
+        nc.sync.dma_start(tab_w[:].bitcast(I32), tab_words[0].rearrange("p t i -> p (t i)").bitcast(I32))
 
+        scan_planes = own("scan_planes", [P, S + H], U8)
+        nc.gpsimd.memset(scan_planes[:].bitcast(I32), 0)
+        v2_planes = [own("v2_plane%d" % a, [P, S], U8) for a in range(2)]
+        for plane in v2_planes:
+            nc.gpsimd.memset(plane[:].bitcast(I32), 0)
+
+        scan_rows = own("scan_rows", [P, S + H], U8)
+        reorder_w4(scan_rows[:, S:S + H], w4_rows[:])
         w4_w = own("w4_w", [P, H], U16)
-        reorder_w4(w4_w, w4_raw)
-        tab_w = staged("area_c", "tab_w", [P, T], U32)
-        for u in range(2):
-            cols = slice(u * T // 2, (u + 1) * T // 2)
-            nc.sync.dma_start(tab_w[:, cols].bitcast(I32),
-                              tab_words[0][:, cols, :].rearrange("p t i -> p (t i)").bitcast(I32))
+        reorder_w4(w4_w[:], w4_raw[:])
+        v_rows = placed(area_a + 8 * KB - S // 2, "v_rows", [P, S], U8)
+        nc.vector.tensor_copy(v_rows[:], tab_rows[:].indirect(list1[:]))
+        nc.vector.tensor_copy(scan_rows[:, 0:S].bitcast(I32), v_rows[:].bitcast(I32))
+        move_rows(scan_planes, scan_rows, P - ROWS)
+        load_tab2(0)
+        load_tab2(1)
 
-        v2_sc0 = own("v2_sc0", [P, S], U8)
-        nc.vector.tensor_copy(v2_sc0[:], tab2_sc[:].indirect(list2[:]))
-        load_w2(0, 0, "area_a")
-        for q in range(QUADRANTS):
-            nc.sync.dma_start(v2_sc1[32 * q:32 * q + 4, :].bitcast(I32),
-                              v2_sc0[32 * q + 4:32 * q + 8, :].bitcast(I32))
-        v2_sc = [v2_sc0, v2_sc1]
-        v_sc = own("v_sc", [P, S], U8)
-        nc.vector.tensor_copy(v_sc[:], tab_sc[:].indirect(list1[:]))
-        load_w2(0, 1, "area_b")
-        w4_sc = own("w4_sc", [P, H], U8)
-        reorder_w4(w4_sc, w4_sc_raw)
+        v2_rows = own("v2_rows", [P, S], U8)
+        nc.vector.tensor_copy(v2_rows[:], tab2_rows[:].indirect(list2[:]))
+        move_rows(v2_planes[0], v2_rows, P - 2 * ROWS)
+        load_w2(0, 1, placed(area_c, "w2_raw01", [P, PACK, PASS], F32))
+        move_rows(v2_planes[1], v2_rows, P - ROWS)
 
-        w2_codes, w2_sc = {}, {}
+        w2_bf, w2_codes, w2_sc = {}, {}, {}
 
-        def quantise_w2(b, a, cast):
-            grouped = staged("w2_bf%d%d" % (b, a), "w2_bf%d%d" % (b, a), [P, PACK * PASS], BF16)
-            cast(grouped[:].rearrange("p (t m j) -> p m j t", t=PACK, j=PACK),
+        def cast_w2(b, a, cast, tile):
+            w2_bf[b, a] = tile
+            cast(tile[:].rearrange("p (t m j) -> p m j t", t=PACK, j=PACK),
                  w2_raw[b, a][:].rearrange("p j (m t) -> p m j t", t=PACK))
-            w2_codes[b, a] = own("w2_codes%d%d" % (b, a), [P, PASS], U32)
-            w2_sc[b, a] = own("w2_sc%d%d" % (b, a), [P, PASS], U8)
-            nc.vector.quantize_mx(out=w2_codes[b, a][:].bitcast(FP8X4), scales=w2_sc[b, a][:], in_=grouped[:])
 
-        def gather_half(name, dtype, window, offsets, h):
-            picked = own(name, [P, HALF], dtype)
+        def quantise_w2(b, a):
+            name = "w2_codes%d%d" % (b, a)
+            w2_codes[b, a] = placed(area_e, name, [P, PASS], U32) if (b, a) == (1, 1) else own(name, [P, PASS], U32)
+            w2_sc[b, a] = own("w2_sc%d%d" % (b, a), [P, PASS], U8)
+            nc.vector.quantize_mx(out=w2_codes[b, a][:].bitcast(FP8X4), scales=w2_sc[b, a][:], in_=w2_bf[b, a][:])
+
+        def gather_half(picked, window, offsets, h):
             nc.vector.tensor_copy(picked[:], window[:].indirect(offsets[:, h * HALF // 16:(h + 1) * HALF // 16]))
             return picked
 
-        v_w = [gather_half("v_w%d" % h, U32, tab_w, list1, h) for h in range(2)]
-        load_tab2(0, "area_c")
-        quantise_w2(0, 0, nc.vector.tensor_copy)
-        load_tab2(1, "area_a")
-        quantise_w2(0, 1, nc.vector.tensor_copy)
-        load_w2(1, 0, "area_b")
-        v2_w = {(0, h): gather_half("v2_w0%d" % h, U16, tab2_w[0], list2, h) for h in range(2)}
-        load_w2(1, 1, "area_c")
-        for h in range(2):
-            v2_w[1, h] = gather_half("v2_w1%d" % h, U16, tab2_w[1], list2, h)
-        load_tw(0, "area_a")
-        quantise_w2(1, 0, nc.scalar.copy)
-        w8_w = staged("area_b", "w8_w", [P, 2 * N], U32)
+        cast_w2(0, 0, nc.scalar.copy, placed(area_d, "w2_bf00", [P, PACK * PASS], BF16))
+        quantise_w2(0, 0)
+        v_w = [gather_half(placed(area_d + 2 * KB * h, "v_w%d" % h, [P, HALF], U32), tab_w, list1, h)
+               for h in range(2)]
+        for a in range(2):
+            load_w2(1, a, placed(area_b + 8 * KB * a, "w2_raw1%d" % a, [P, PACK, PASS], F32))
+        v2_w = {}
+        for a in range(2):
+            for h in range(2):
+                v2_w[a, h] = gather_half(own("v2_w%d%d" % (a, h), [P, HALF], U16), tab2_w[a], list2, h)
+            load_tw(a)
+        cast_w2(0, 1, nc.vector.tensor_copy, own("w2_bf01", [P, PACK * PASS], BF16))
+        quantise_w2(0, 1)
+        w8_w = placed(area_c, "w8_w", [P, 2 * N], U32)
         nc.sync.dma_start(w8_w[:].bitcast(I32).rearrange("p (b c) -> p b c", b=2),
                           w8_words.rearrange("b p c i -> p b (c i)").bitcast(I32))
-        w8_sc = staged("w2_bf10", "w8_sc", [P, N], U8)
-        load_scales(nc.gpsimd, w8_sc, w8_scales)
-        quantise_w2(1, 1, nc.scalar.copy)
-        load_tw(1, "area_c")
+        w8_sc = placed(area_c + 4 * KB, "w8_sc", [P, N], U8)
+        nc.gpsimd.memset(w8_sc[:].bitcast(I32), 0)
+        for q in range(QUADRANTS):
+            nc.sync.dma_start(w8_sc[32 * q:32 * q + 8, :].bitcast(I32), w8_scales[:, 4 * q:4 * q + 4, :].bitcast(I32))
 
         scan_sb, diff, gap_codes, gap_sc = {}, {}, {}, {}
+        banks_used = []
+
+        def next_bank(name, shape):
+            banks_used.append(name)
+            return psum.tile(shape, F32, name=name, tag="bank%d" % (len(banks_used) % BANKS), bufs=1)
 
         def scan_block(b, h):
             for t in range(PACK):
-                acc = psum.tile([P, HALF], F32, name="scan_ps", tag="scan_then_y", bufs=BANKS)
+                acc = next_bank("scan_ps", [P, HALF])
                 cols = slice(PASS * b + P * t, PASS * b + P * (t + 1))
-                nc.tensor.matmul_mx(out=acc[:], lhsT=w4_w[:, cols].bitcast(FP4X4), lhsT_scale=w4_sc[:, cols],
-                                    rhs=v_w[h][:].bitcast(FP8X4), rhs_scale=v_sc[:, h * HALF:(h + 1) * HALF],
+                nc.tensor.matmul_mx(out=acc[:], lhsT=w4_w[:, cols].bitcast(FP4X4),
+                                    lhsT_scale=scan_planes[:, S + cols.start:S + cols.stop],
+                                    rhs=v_w[h][:].bitcast(FP8X4), rhs_scale=scan_planes[:, h * HALF:(h + 1) * HALF],
                                     start=True, stop=True)
-                scan_sb[b, h, t] = own("scan%d%d%d" % (b, h, t), [P, HALF], F32)
+                name = "scan%d%d%d" % (b, h, t)
+                scan_sb[b, h, t] = placed(area_e + 4 * KB * t, name, [P, HALF], F32) if (b, h) == (0, 0) else own(
+                    name, [P, HALF], F32)
                 nc.scalar.copy(scan_sb[b, h, t][:], acc[:])
 
         def old_block(b, h):
             diff[b, h] = own("diff%d%d" % (b, h), [P, PACK, HALF], BF16)
             for t in range(PACK):
-                acc = psum.tile([P, HALF], F32, name="old_ps", tag="old", bufs=BANKS)
+                acc = next_bank("old_ps", [P, HALF])
                 cols = slice(P * t, P * (t + 1))
-                for a in range(2):
+                for a in (1, 0):
                     nc.tensor.matmul_mx(out=acc[:], lhsT=w2_codes[b, a][:, cols].bitcast(FP8X4),
                                         lhsT_scale=w2_sc[b, a][:, cols], rhs=v2_w[a, h][:].bitcast(FP4X4),
-                                        rhs_scale=v2_sc[a][:, h * HALF:(h + 1) * HALF], start=(a == 0), stop=(a == 1))
+                                        rhs_scale=v2_planes[a][:, h * HALF:(h + 1) * HALF],
+                                        start=(a == 1), stop=(a == 0))
                 nc.vector.tensor_tensor(diff[b, h][:, t, :], acc[:], scan_sb[b, h, t][:], ALU.subtract)
 
         def gap_piece(b, f):
@@ -172,15 +195,15 @@ def tile_list_map_change_gap_kernel(tc, tab_words, tab_scales, tab2_words, tab2_
         def final_piece(f):
             h, col = divmod(f * PIECE, HALF)
             for g in range(2):
-                acc = psum.tile([P, 2, PIECE], F32, name="y_ps", tag="scan_then_y", bufs=BANKS)
+                acc = next_bank("y_ps", [P, 2, PIECE])
                 for i in range(2):
                     first = P * (2 * g + i)
-                    for b in range(2):
+                    for b in (1, 0):
                         nc.tensor.matmul_mx(out=acc[:, i, :],
                                             lhsT=w8_w[:, N * b + first:N * b + first + P].bitcast(FP8X4),
                                             lhsT_scale=w8_sc[4 * b:P, first:first + P],
                                             rhs=gap_codes[b, f][:].bitcast(FP8X4), rhs_scale=gap_sc[b, f][:],
-                                            start=(b == 0), stop=(b == 1))
+                                            start=(b == 1), stop=(b == 0))
                 weighted = own("weighted%d%d" % (f, g), [P, 2, PIECE], F32)
                 nc.vector.tensor_tensor(weighted[:], acc[:], tw_sb[h][:, 2 * g:2 * g + 2, col:col + PIECE], ALU.mult)
                 res = own("res%d%d" % (f, g), [P, 2, PIECE], F32)
@@ -189,13 +212,20 @@ def tile_list_map_change_gap_kernel(tc, tab_words, tab_scales, tab2_words, tab2_
                     out[2 * P * g:2 * P * (g + 1), PIECE * f:PIECE * (f + 1)].rearrange("(i p) s -> p i s", p=P),
                     res[:])
 
-        for b in range(2):
-            for h in range(2):
-                scan_block(b, h)
-            for h in range(2):
-                old_block(b, h)
-        for f in range(S // PIECE):
+        for h in range(2):
             for b in range(2):
-                gap_piece(b, f)
+                scan_block(b, h)
+        old_block(0, 0)
+        cast_w2(1, 0, nc.scalar.copy, placed(area_e, "w2_bf10", [P, PACK * PASS], BF16))
+        cast_w2(1, 1, nc.vector.tensor_copy, placed(area_e + 12 * KB, "w2_bf11", [P, PACK * PASS], BF16))
+        quantise_w2(1, 0)
+        quantise_w2(1, 1)
+        old_block(0, 1)
+        for h in range(2):
+            old_block(1, h)
+        for f in range(S // PIECE):
+            gap_piece(0, f)
+        for f in range(S // PIECE):
+            gap_piece(1, f)
         for f in range(S // PIECE):
             final_piece(f)

@@ -22,7 +22,6 @@ PASS = P * PACK
 QUADRANTS = 4
 ROWS = 16
 HALF = S // 2
-PIECE = 256
 RUN = 4
 BANKS = 8
 KB = 1024
@@ -42,7 +41,7 @@ def tile_list_map_change_gap_kernel(tc, tab_words, tab_scales, tab2_words, tab2_
         def placed(offset, name, shape, dtype):
             return shared.tile(shape, dtype, name=name, align_bytes=64, offset=offset)
 
-        area_a, area_b, area_c, area_d, area_e = 0, 16 * KB, 32 * KB, 40 * KB, 44 * KB
+        area_a, area_b, area_c, area_d, area_e, area_f = 0, 16 * KB, 32 * KB, 40 * KB, 44 * KB, 60 * KB
 
         list1 = keep.tile([P, S // 16], U16, name="list1")
         list2 = keep.tile([P, S // 16], U16, name="list2")
@@ -57,9 +56,9 @@ def tile_list_map_change_gap_kernel(tc, tab_words, tab_scales, tab2_words, tab2_
             tab2_w[a] = placed(area_a + 8 * KB * a, "tab2_w%d" % a, [P, T], U16)
             nc.sync.dma_start(tab2_w[a][:].bitcast(I32), tab2_words[a].bitcast(I32))
 
-        def load_tw(h):
-            tw_sb[h] = placed(area_a + 8 * KB * h, "tw%d" % h, [P, N // P, HALF], F32)
-            nc.sync.dma_start(tw_sb[h][:], tw[:, HALF * h:HALF * (h + 1)].rearrange("(nt p) s -> p nt s", p=P))
+        def load_tw(g):
+            tw_sb[g] = placed(area_a + 8 * KB * g, "tw%d" % g, [P, 2, S], F32)
+            nc.sync.dma_start(tw_sb[g][:], tw[2 * P * g:2 * P * (g + 1), :].rearrange("(i p) s -> p i s", p=P))
 
         def load_rows(tile, scales, clearing_engine):
             rows = scales.rearrange("a q c -> (a q) c")
@@ -85,16 +84,16 @@ def tile_list_map_change_gap_kernel(tc, tab_words, tab_scales, tab2_words, tab2_
         load_rows(tab_rows, tab_scales, nc.vector)
         nc.sync.dma_start(list2[:], offs2)
         tab2_rows = placed(area_c, "tab2_rows", [P, T], U8)
-        load_rows(tab2_rows, tab2_scales, nc.gpsimd)
+        load_rows(tab2_rows, tab2_scales, nc.vector)
         load_w2(0, 0, own("w2_raw00", [P, PACK, PASS], F32))
         tab_w = placed(area_b, "tab_w", [P, T], U32)
         nc.sync.dma_start(tab_w[:].bitcast(I32), tab_words[0].rearrange("p t i -> p (t i)").bitcast(I32))
 
         scan_planes = own("scan_planes", [P, S + H], U8)
-        nc.gpsimd.memset(scan_planes[:].bitcast(I32), 0)
+        nc.vector.memset(scan_planes[:].bitcast(I32), 0)
         v2_planes = [own("v2_plane%d" % a, [P, S], U8) for a in range(2)]
         for plane in v2_planes:
-            nc.gpsimd.memset(plane[:].bitcast(I32), 0)
+            nc.vector.memset(plane[:].bitcast(I32), 0)
 
         scan_rows = own("scan_rows", [P, S + H], U8)
         reorder_w4(scan_rows[:, S:S + H], w4_rows[:])
@@ -137,21 +136,23 @@ def tile_list_map_change_gap_kernel(tc, tab_words, tab_scales, tab2_words, tab2_
         for a in range(2):
             load_w2(1, a, placed(area_b + 8 * KB * a, "w2_raw1%d" % a, [P, PACK, PASS], F32))
         v2_w = {}
-        for a in range(2):
-            for h in range(2):
-                v2_w[a, h] = gather_half(own("v2_w%d%d" % (a, h), [P, HALF], U16), tab2_w[a], list2, h)
-            load_tw(a)
-        cast_w2(0, 1, nc.vector.tensor_copy, own("w2_bf01", [P, PACK * PASS], BF16))
+        for h in range(2):
+            v2_w[0, h] = gather_half(own("v2_w0%d" % h, [P, HALF], U16), tab2_w[0], list2, h)
+        load_tw(0)
+        v2_w[1, 0] = gather_half(own("v2_w10", [P, HALF], U16), tab2_w[1], list2, 0)
+        cast_w2(0, 1, nc.vector.tensor_copy, placed(area_f, "w2_bf01", [P, PACK * PASS], BF16))
         quantise_w2(0, 1)
+        v2_w[1, 1] = gather_half(placed(area_f, "v2_w11", [P, HALF], U16), tab2_w[1], list2, 1)
+        load_tw(1)
         w8_w = placed(area_c, "w8_w", [P, 2 * N], U32)
         nc.sync.dma_start(w8_w[:].bitcast(I32).rearrange("p (b c) -> p b c", b=2),
                           w8_words.rearrange("b p c i -> p b (c i)").bitcast(I32))
         w8_sc = placed(area_c + 4 * KB, "w8_sc", [P, N], U8)
-        nc.gpsimd.memset(w8_sc[:].bitcast(I32), 0)
+        nc.vector.memset(w8_sc[:].bitcast(I32), 0)
         for q in range(QUADRANTS):
             nc.sync.dma_start(w8_sc[32 * q:32 * q + 8, :].bitcast(I32), w8_scales[:, 4 * q:4 * q + 4, :].bitcast(I32))
 
-        scan_sb, diff, gap_codes, gap_sc = {}, {}, {}, {}
+        scan_sb, diff, gap, gap_codes, gap_sc, weighted = {}, {}, {}, {}, {}, {}
         banks_used = []
 
         def next_bank(name, shape):
@@ -183,34 +184,31 @@ def tile_list_map_change_gap_kernel(tc, tab_words, tab_scales, tab2_words, tab2_
                                         start=(a == 1), stop=(a == 0))
                 nc.vector.tensor_tensor(diff[b, h][:, t, :], acc[:], scan_sb[b, h, t][:], ALU.subtract)
 
-        def gap_piece(b, f):
-            gap = own("gap%d%d" % (b, f), [P, PIECE * PACK], BF16)
-            h, col = divmod(f * PIECE, HALF)
-            nc.scalar.activation(gap[:].rearrange("p (c i t) -> p c t i", i=RUN, t=PACK),
-                                 diff[b, h][:, :, col:col + PIECE].rearrange("p t (c i) -> p c t i", i=RUN), ABS)
-            gap_codes[b, f] = own("gap_codes%d%d" % (b, f), [P, PIECE], U32)
-            gap_sc[b, f] = own("gap_sc%d%d" % (b, f), [P, PIECE], U8)
-            nc.vector.quantize_mx(out=gap_codes[b, f][:].bitcast(FP8X4), scales=gap_sc[b, f][:], in_=gap[:])
+        def magnitudes(b, h):
+            gap[b, h] = own("gap%d%d" % (b, h), [P, HALF * PACK], BF16)
+            nc.scalar.activation(gap[b, h][:].rearrange("p (c i t) -> p c t i", i=RUN, t=PACK),
+                                 diff[b, h][:].rearrange("p t (c i) -> p c t i", i=RUN), ABS)
 
-        def final_piece(f):
-            h, col = divmod(f * PIECE, HALF)
-            for g in range(2):
-                acc = next_bank("y_ps", [P, 2, PIECE])
-                for i in range(2):
-                    first = P * (2 * g + i)
-                    for b in (1, 0):
-                        nc.tensor.matmul_mx(out=acc[:, i, :],
-                                            lhsT=w8_w[:, N * b + first:N * b + first + P].bitcast(FP8X4),
-                                            lhsT_scale=w8_sc[4 * b:P, first:first + P],
-                                            rhs=gap_codes[b, f][:].bitcast(FP8X4), rhs_scale=gap_sc[b, f][:],
-                                            start=(b == 1), stop=(b == 0))
-                weighted = own("weighted%d%d" % (f, g), [P, 2, PIECE], F32)
-                nc.vector.tensor_tensor(weighted[:], acc[:], tw_sb[h][:, 2 * g:2 * g + 2, col:col + PIECE], ALU.mult)
-                res = own("res%d%d" % (f, g), [P, 2, PIECE], F32)
-                nc.scalar.activation(res[:], weighted[:], ABS)
-                nc.sync.dma_start(
-                    out[2 * P * g:2 * P * (g + 1), PIECE * f:PIECE * (f + 1)].rearrange("(i p) s -> p i s", p=P),
-                    res[:])
+        def quantise_gap(b, h):
+            gap_codes[b, h] = own("gap_codes%d%d" % (b, h), [P, HALF], U32)
+            gap_sc[b, h] = own("gap_sc%d%d" % (b, h), [P, HALF], U8)
+            nc.vector.quantize_mx(out=gap_codes[b, h][:].bitcast(FP8X4), scales=gap_sc[b, h][:], in_=gap[b, h][:])
+
+        def weigh(h, nt):
+            acc = next_bank("y_ps", [P, HALF])
+            for b in (1, 0):
+                nc.tensor.matmul_mx(out=acc[:], lhsT=w8_w[:, N * b + P * nt:N * b + P * (nt + 1)].bitcast(FP8X4),
+                                    lhsT_scale=w8_sc[4 * b:P, P * nt:P * (nt + 1)],
+                                    rhs=gap_codes[b, h][:].bitcast(FP8X4), rhs_scale=gap_sc[b, h][:],
+                                    start=(b == 1), stop=(b == 0))
+            weighted[h, nt] = own("weighted%d%d" % (h, nt), [P, HALF], F32)
+            nc.vector.tensor_tensor(weighted[h, nt][:], acc[:], tw_sb[nt // 2][:, nt % 2, h * HALF:(h + 1) * HALF],
+                                    ALU.mult)
+
+        def store(h, nt):
+            res = own("res%d%d" % (h, nt), [P, HALF], F32)
+            nc.scalar.activation(res[:], weighted[h, nt][:], ABS)
+            nc.sync.dma_start(out[P * nt:P * (nt + 1), HALF * h:HALF * (h + 1)], res[:])
 
         for h in range(2):
             for b in range(2):
@@ -223,9 +221,19 @@ def tile_list_map_change_gap_kernel(tc, tab_words, tab_scales, tab2_words, tab2_
         old_block(0, 1)
         for h in range(2):
             old_block(1, h)
-        for f in range(S // PIECE):
-            gap_piece(0, f)
-        for f in range(S // PIECE):
-            gap_piece(1, f)
-        for f in range(S // PIECE):
-            final_piece(f)
+        for b in range(2):
+            for h in range(2):
+                magnitudes(b, h)
+        quantise_gap(0, 0)
+        quantise_gap(1, 0)
+        quantise_gap(0, 1)
+        weigh(0, 0)
+        weigh(0, 1)
+        quantise_gap(1, 1)
+        weigh(0, 2)
+        weigh(0, 3)
+        for nt in range(N // P):
+            weigh(1, nt)
+        for h in range(2):
+            for nt in range(N // P):
+                store(h, nt)

@@ -53,7 +53,7 @@ def tile_list_map_change_gap_kernel(tc, tab_words, tab_scales, tab2_words, tab2_
                 tile[:], w2[PASS * a:PASS * (a + 1), PASS * b:PASS * (b + 1)].rearrange("(p j) c -> p j c", j=PACK))
 
         def load_tab2(a):
-            tab2_w[a] = placed(area_a + 8 * KB * a, "tab2_w%d" % a, [P, T], U16)
+            tab2_w[a] = placed((area_a, area_c)[a], "tab2_w%d" % a, [P, T], U16)
             nc.sync.dma_start(tab2_w[a][:].bitcast(I32), tab2_words[a].bitcast(I32))
 
         def load_tw(g):
@@ -104,20 +104,20 @@ def tile_list_map_change_gap_kernel(tc, tab_words, tab_scales, tab2_words, tab2_
         nc.vector.tensor_copy(scan_rows[:, 0:S].bitcast(I32), v_rows[:].bitcast(I32))
         move_rows(scan_planes, scan_rows, P - ROWS)
         load_tab2(0)
-        load_tab2(1)
+        load_w2(0, 1, placed(area_a + 8 * KB, "w2_raw01", [P, PACK, PASS], F32))
 
         v2_rows = own("v2_rows", [P, S], U8)
         nc.vector.tensor_copy(v2_rows[:], tab2_rows[:].indirect(list2[:]))
         move_rows(v2_planes[0], v2_rows, P - 2 * ROWS)
-        load_w2(0, 1, placed(area_c, "w2_raw01", [P, PACK, PASS], F32))
+        load_tab2(1)
         move_rows(v2_planes[1], v2_rows, P - ROWS)
 
         w2_bf, w2_codes, w2_sc = {}, {}, {}
 
         def cast_w2(b, a, cast, tile):
             w2_bf[b, a] = tile
-            cast(tile[:].rearrange("p (t m j) -> p m j t", t=PACK, j=PACK),
-                 w2_raw[b, a][:].rearrange("p j (m t) -> p m j t", t=PACK))
+            cast(tile[:].rearrange("p (t m j) -> p m t j", t=PACK, j=PACK),
+                 w2_raw[b, a][:].rearrange("p j (m t) -> p m t j", t=PACK))
 
         def quantise_w2(b, a):
             name = "w2_codes%d%d" % (b, a)
@@ -139,11 +139,11 @@ def tile_list_map_change_gap_kernel(tc, tab_words, tab_scales, tab2_words, tab2_
         for h in range(2):
             v2_w[0, h] = gather_half(own("v2_w0%d" % h, [P, HALF], U16), tab2_w[0], list2, h)
         load_tw(0)
-        v2_w[1, 0] = gather_half(own("v2_w10", [P, HALF], U16), tab2_w[1], list2, 0)
         cast_w2(0, 1, nc.vector.tensor_copy, placed(area_f, "w2_bf01", [P, PACK * PASS], BF16))
-        quantise_w2(0, 1)
-        v2_w[1, 1] = gather_half(placed(area_f, "v2_w11", [P, HALF], U16), tab2_w[1], list2, 1)
         load_tw(1)
+        quantise_w2(0, 1)
+        for h in range(2):
+            v2_w[1, h] = gather_half(placed(area_f + KB * h, "v2_w1%d" % h, [P, HALF], U16), tab2_w[1], list2, h)
         w8_w = placed(area_c, "w8_w", [P, 2 * N], U32)
         nc.sync.dma_start(w8_w[:].bitcast(I32).rearrange("p (b c) -> p b c", b=2),
                           w8_words.rearrange("b p c i -> p b (c i)").bitcast(I32))
@@ -159,6 +159,8 @@ def tile_list_map_change_gap_kernel(tc, tab_words, tab_scales, tab2_words, tab2_
             banks_used.append(name)
             return psum.tile(shape, F32, name=name, tag="bank%d" % (len(banks_used) % BANKS), bufs=1)
 
+        shared_scans = {(0, 0, 0): area_e, (0, 1, 1): area_e + 12 * KB}
+
         def scan_block(b, h):
             for t in range(PACK):
                 acc = next_bank("scan_ps", [P, HALF])
@@ -168,13 +170,14 @@ def tile_list_map_change_gap_kernel(tc, tab_words, tab_scales, tab2_words, tab2_
                                     rhs=v_w[h][:].bitcast(FP8X4), rhs_scale=scan_planes[:, h * HALF:(h + 1) * HALF],
                                     start=True, stop=True)
                 name = "scan%d%d%d" % (b, h, t)
-                scan_sb[b, h, t] = placed(area_e + 4 * KB * t, name, [P, HALF], F32) if (b, h) == (0, 0) else own(
+                scan_sb[b, h, t] = placed(shared_scans[b, h, t], name, [P, HALF], F32) if (b, h, t) in shared_scans else own(
                     name, [P, HALF], F32)
                 nc.scalar.copy(scan_sb[b, h, t][:], acc[:])
 
-        def old_block(b, h):
-            diff[b, h] = own("diff%d%d" % (b, h), [P, PACK, HALF], BF16)
-            for t in range(PACK):
+        def old_block(b, h, rows=range(PACK)):
+            if (b, h) not in diff:
+                diff[b, h] = own("diff%d%d" % (b, h), [P, PACK, HALF], BF16)
+            for t in rows:
                 acc = next_bank("old_ps", [P, HALF])
                 cols = slice(P * t, P * (t + 1))
                 for a in (1, 0):
@@ -214,11 +217,12 @@ def tile_list_map_change_gap_kernel(tc, tab_words, tab_scales, tab2_words, tab2_
             for b in range(2):
                 scan_block(b, h)
         old_block(0, 0)
+        old_block(0, 1, range(2))
         cast_w2(1, 0, nc.scalar.copy, placed(area_e, "w2_bf10", [P, PACK * PASS], BF16))
         cast_w2(1, 1, nc.vector.tensor_copy, placed(area_e + 12 * KB, "w2_bf11", [P, PACK * PASS], BF16))
         quantise_w2(1, 0)
         quantise_w2(1, 1)
-        old_block(0, 1)
+        old_block(0, 1, range(2, PACK))
         for h in range(2):
             old_block(1, h)
         for b in range(2):

@@ -23,7 +23,6 @@ QUADRANTS = 4
 ROWS = 16
 HALF = S // 2
 RUN = 4
-BANKS = 8
 KB = 1024
 
 
@@ -41,7 +40,8 @@ def tile_list_map_change_gap_kernel(tc, tab_words, tab_scales, tab2_words, tab2_
         def placed(offset, name, shape, dtype):
             return shared.tile(shape, dtype, name=name, align_bytes=64, offset=offset)
 
-        area_a, area_b, area_c, area_d, area_e, area_f = 0, 16 * KB, 32 * KB, 40 * KB, 44 * KB, 60 * KB
+        area_a, area_b, area_c, area_d, area_e, area_f, area_g = (
+            0, 16 * KB, 32 * KB, 40 * KB, 44 * KB, 60 * KB, 64 * KB)
 
         list1 = keep.tile([P, S // 16], U16, name="list1")
         list2 = keep.tile([P, S // 16], U16, name="list2")
@@ -121,7 +121,8 @@ def tile_list_map_change_gap_kernel(tc, tab_words, tab_scales, tab2_words, tab2_
 
         def quantise_w2(b, a):
             name = "w2_codes%d%d" % (b, a)
-            w2_codes[b, a] = placed(area_e, name, [P, PASS], U32) if (b, a) == (1, 1) else own(name, [P, PASS], U32)
+            w2_codes[b, a] = placed(area_e + 8 * KB, name, [P, PASS], U32) if (b, a) == (1, 0) else own(
+                name, [P, PASS], U32)
             w2_sc[b, a] = own("w2_sc%d%d" % (b, a), [P, PASS], U8)
             nc.vector.quantize_mx(out=w2_codes[b, a][:].bitcast(FP8X4), scales=w2_sc[b, a][:], in_=w2_bf[b, a][:])
 
@@ -153,17 +154,17 @@ def tile_list_map_change_gap_kernel(tc, tab_words, tab_scales, tab2_words, tab2_
             nc.sync.dma_start(w8_sc[32 * q:32 * q + 8, :].bitcast(I32), w8_scales[:, 4 * q:4 * q + 4, :].bitcast(I32))
 
         scan_sb, diff, gap, gap_codes, gap_sc, weighted = {}, {}, {}, {}, {}, {}
-        banks_used = []
 
-        def next_bank(name, shape):
-            banks_used.append(name)
-            return psum.tile(shape, F32, name=name, tag="bank%d" % (len(banks_used) % BANKS), bufs=1)
+        def bank(index, name):
+            return psum.tile([P, HALF], F32, name=name, tag="bank%d" % index, bufs=1)
 
-        shared_scans = {(0, 0, 0): area_e, (0, 1, 1): area_e + 12 * KB}
+        shared_scans = {(0, 0, 0): area_e, (0, 1, 1): area_e + 8 * KB, (1, 1, 2): area_e + 12 * KB}
+        old_banks = {(0, 0): (4, 5, 6, 7), (0, 1): (0, 1, 2, 3), (1, 0): (4, 5, 6, 7), (1, 1): (5, 6, 7, 5)}
+        y_banks = ((0, 1, 2, 3), (4, 6, 7, 5))
 
         def scan_block(b, h):
             for t in range(PACK):
-                acc = next_bank("scan_ps", [P, HALF])
+                acc = bank(t, "scan_ps")
                 cols = slice(PASS * b + P * t, PASS * b + P * (t + 1))
                 nc.tensor.matmul_mx(out=acc[:], lhsT=w4_w[:, cols].bitcast(FP4X4),
                                     lhsT_scale=scan_planes[:, S + cols.start:S + cols.stop],
@@ -178,32 +179,36 @@ def tile_list_map_change_gap_kernel(tc, tab_words, tab_scales, tab2_words, tab2_
             if (b, h) not in diff:
                 diff[b, h] = own("diff%d%d" % (b, h), [P, PACK, HALF], BF16)
             for t in rows:
-                acc = next_bank("old_ps", [P, HALF])
+                acc = bank(old_banks[b, h][t], "old_ps")
                 cols = slice(P * t, P * (t + 1))
-                for a in (1, 0):
+                for a in (b ^ 1, b):
                     nc.tensor.matmul_mx(out=acc[:], lhsT=w2_codes[b, a][:, cols].bitcast(FP8X4),
                                         lhsT_scale=w2_sc[b, a][:, cols], rhs=v2_w[a, h][:].bitcast(FP4X4),
                                         rhs_scale=v2_planes[a][:, h * HALF:(h + 1) * HALF],
-                                        start=(a == 1), stop=(a == 0))
+                                        start=(a != b), stop=(a == b))
                 nc.vector.tensor_tensor(diff[b, h][:, t, :], acc[:], scan_sb[b, h, t][:], ALU.subtract)
 
         def magnitudes(b, h):
-            gap[b, h] = own("gap%d%d" % (b, h), [P, HALF * PACK], BF16)
+            name = "gap%d%d" % (b, h)
+            gap[b, h] = placed(area_g, name, [P, HALF * PACK], BF16) if (b, h) == (1, 0) else own(
+                name, [P, HALF * PACK], BF16)
             nc.scalar.activation(gap[b, h][:].rearrange("p (c i t) -> p c t i", i=RUN, t=PACK),
                                  diff[b, h][:].rearrange("p t (c i) -> p c t i", i=RUN), ABS)
 
         def quantise_gap(b, h):
-            gap_codes[b, h] = own("gap_codes%d%d" % (b, h), [P, HALF], U32)
+            name = "gap_codes%d%d" % (b, h)
+            gap_codes[b, h] = placed((area_e + 12 * KB, area_g)[h], name, [P, HALF], U32) if b == 0 else own(
+                name, [P, HALF], U32)
             gap_sc[b, h] = own("gap_sc%d%d" % (b, h), [P, HALF], U8)
             nc.vector.quantize_mx(out=gap_codes[b, h][:].bitcast(FP8X4), scales=gap_sc[b, h][:], in_=gap[b, h][:])
 
         def weigh(h, nt):
-            acc = next_bank("y_ps", [P, HALF])
-            for b in (1, 0):
+            acc = bank(y_banks[h][nt], "y_ps")
+            for b in range(2):
                 nc.tensor.matmul_mx(out=acc[:], lhsT=w8_w[:, N * b + P * nt:N * b + P * (nt + 1)].bitcast(FP8X4),
                                     lhsT_scale=w8_sc[4 * b:P, P * nt:P * (nt + 1)],
                                     rhs=gap_codes[b, h][:].bitcast(FP8X4), rhs_scale=gap_sc[b, h][:],
-                                    start=(b == 1), stop=(b == 0))
+                                    start=(b == 0), stop=(b == 1))
             weighted[h, nt] = own("weighted%d%d" % (h, nt), [P, HALF], F32)
             nc.vector.tensor_tensor(weighted[h, nt][:], acc[:], tw_sb[nt // 2][:, nt % 2, h * HALF:(h + 1) * HALF],
                                     ALU.mult)
@@ -219,16 +224,18 @@ def tile_list_map_change_gap_kernel(tc, tab_words, tab_scales, tab2_words, tab2_
         old_block(0, 0)
         old_block(0, 1, range(2))
         cast_w2(1, 0, nc.scalar.copy, placed(area_e, "w2_bf10", [P, PACK * PASS], BF16))
-        cast_w2(1, 1, nc.vector.tensor_copy, placed(area_e + 12 * KB, "w2_bf11", [P, PACK * PASS], BF16))
         quantise_w2(1, 0)
+        cast_w2(1, 1, nc.vector.tensor_copy, placed(area_e, "w2_bf11", [P, PACK * PASS], BF16))
         quantise_w2(1, 1)
         old_block(0, 1, range(2, PACK))
         for h in range(2):
-            old_block(1, h)
-        for b in range(2):
-            for h in range(2):
-                magnitudes(b, h)
+            magnitudes(0, h)
+        old_block(1, 0)
+        magnitudes(1, 0)
+        old_block(1, 1, range(PACK - 1))
         quantise_gap(0, 0)
+        old_block(1, 1, range(PACK - 1, PACK))
+        magnitudes(1, 1)
         quantise_gap(1, 0)
         quantise_gap(0, 1)
         weigh(0, 0)

@@ -66,8 +66,8 @@ def tile_list_map_change_gap_kernel(tc, tab_words, tab_scales, tab2_words, tab2_
             nc.sync.dma_start(tile[first:P, :].bitcast(I32), rows.bitcast(I32))
             clearing_engine.memset(tile[0:first, :].bitcast(I32), 0)
 
-        def move_rows(plane, rows, first):
-            for q in range(QUADRANTS):
+        def move_rows(plane, rows, first, quadrants=range(QUADRANTS)):
+            for q in quadrants:
                 nc.sync.dma_start(plane[32 * q:32 * q + 4, :].bitcast(I32),
                                   rows[first + 4 * q:first + 4 * q + 4, :].bitcast(I32))
 
@@ -108,20 +108,21 @@ def tile_list_map_change_gap_kernel(tc, tab_words, tab_scales, tab2_words, tab2_
 
         v2_rows = own("v2_rows", [P, S], U8)
         nc.vector.tensor_copy(v2_rows[:], tab2_rows[:].indirect(list2[:]))
-        move_rows(v2_planes[0], v2_rows, P - 2 * ROWS)
+        move_rows(v2_planes[0], v2_rows, P - 2 * ROWS, range(2))
         load_tab2(1)
+        move_rows(v2_planes[0], v2_rows, P - 2 * ROWS, range(2, QUADRANTS))
         move_rows(v2_planes[1], v2_rows, P - ROWS)
 
         w2_bf, w2_codes, w2_sc = {}, {}, {}
 
-        def cast_w2(b, a, cast, tile):
+        def cast_w2(b, a, cast, tile, part=slice(0, PACK)):
             w2_bf[b, a] = tile
-            cast(tile[:].rearrange("p (t m j) -> p m t j", t=PACK, j=PACK),
-                 w2_raw[b, a][:].rearrange("p j (m t) -> p m t j", t=PACK))
+            cast(tile[:, PASS * part.start:PASS * part.stop].rearrange("p (t m j) -> p m t j", m=P, j=PACK),
+                 w2_raw[b, a][:].rearrange("p j (m t) -> p m t j", t=PACK)[:, :, part, :])
 
         def quantise_w2(b, a):
             name = "w2_codes%d%d" % (b, a)
-            w2_codes[b, a] = placed(area_e + 8 * KB, name, [P, PASS], U32) if (b, a) == (1, 0) else own(
+            w2_codes[b, a] = placed(area_e + (8 + 2 * a) * KB, name, [P, PASS], U32) if b == 1 else own(
                 name, [P, PASS], U32)
             w2_sc[b, a] = own("w2_sc%d%d" % (b, a), [P, PASS], U8)
             nc.vector.quantize_mx(out=w2_codes[b, a][:].bitcast(FP8X4), scales=w2_sc[b, a][:], in_=w2_bf[b, a][:])
@@ -158,7 +159,8 @@ def tile_list_map_change_gap_kernel(tc, tab_words, tab_scales, tab2_words, tab2_
         def bank(index, name):
             return psum.tile([P, HALF], F32, name=name, tag="bank%d" % index, bufs=1)
 
-        shared_scans = {(0, 0, 0): area_e, (0, 1, 1): area_e + 8 * KB, (1, 1, 2): area_e + 12 * KB}
+        shared_scans = {(0, 0, 2): area_e, (0, 0, 3): area_e + 4 * KB, (0, 1, 0): area_e + 8 * KB,
+                        (0, 1, 2): area_e + 10 * KB, (1, 1, 2): area_e + 12 * KB}
         old_banks = {(0, 0): (4, 5, 6, 7), (0, 1): (0, 1, 2, 3), (1, 0): (4, 5, 6, 7), (1, 1): (5, 6, 7, 5)}
         y_banks = ((0, 1, 2, 3), (4, 6, 7, 5))
 
@@ -190,7 +192,7 @@ def tile_list_map_change_gap_kernel(tc, tab_words, tab_scales, tab2_words, tab2_
 
         def magnitudes(b, h):
             name = "gap%d%d" % (b, h)
-            gap[b, h] = placed(area_g, name, [P, HALF * PACK], BF16) if (b, h) == (1, 0) else own(
+            gap[b, h] = placed((area_b + 8 * KB, area_g)[b], name, [P, HALF * PACK], BF16) if h == 0 else own(
                 name, [P, HALF * PACK], BF16)
             nc.scalar.activation(gap[b, h][:].rearrange("p (c i t) -> p c t i", i=RUN, t=PACK),
                                  diff[b, h][:].rearrange("p t (c i) -> p c t i", i=RUN), ABS)
@@ -222,12 +224,15 @@ def tile_list_map_change_gap_kernel(tc, tab_words, tab_scales, tab2_words, tab2_
             for b in range(2):
                 scan_block(b, h)
         old_block(0, 0)
-        old_block(0, 1, range(2))
-        cast_w2(1, 0, nc.scalar.copy, placed(area_e, "w2_bf10", [P, PACK * PASS], BF16))
+        w2_bf10 = placed(area_e, "w2_bf10", [P, PACK * PASS], BF16)
+        cast_w2(1, 0, nc.vector.tensor_copy, w2_bf10, slice(0, PACK // 2))
+        cast_w2(1, 0, nc.scalar.copy, w2_bf10, slice(PACK // 2, PACK))
+        cast_w2(1, 1, nc.scalar.copy, placed(area_e + 4 * KB, "w2_bf11", [P, PACK * PASS], BF16))
+        old_block(0, 1, range(1))
         quantise_w2(1, 0)
-        cast_w2(1, 1, nc.vector.tensor_copy, placed(area_e, "w2_bf11", [P, PACK * PASS], BF16))
+        old_block(0, 1, range(1, PACK - 1))
         quantise_w2(1, 1)
-        old_block(0, 1, range(2, PACK))
+        old_block(0, 1, range(PACK - 1, PACK))
         for h in range(2):
             magnitudes(0, h)
         old_block(1, 0)

@@ -57,7 +57,7 @@ def tile_list_map_change_gap_kernel(tc, tab_words, tab_scales, tab2_words, tab2_
             nc.sync.dma_start(tab2_w[a][:].bitcast(I32), tab2_words[a].bitcast(I32))
 
         def load_tw(g):
-            tw_sb[g] = placed(area_a + 8 * KB * g, "tw%d" % g, [P, 2, S], F32)
+            tw_sb[g] = placed((area_a + 8 * KB, area_c)[g], "tw%d" % g, [P, 2, S], F32)
             nc.sync.dma_start(tw_sb[g][:], tw[2 * P * g:2 * P * (g + 1), :].rearrange("(i p) s -> p i s", p=P))
 
         def load_rows(tile, scales, clearing_engine):
@@ -68,8 +68,7 @@ def tile_list_map_change_gap_kernel(tc, tab_words, tab_scales, tab2_words, tab2_
 
         def move_rows(plane, rows, first, quadrants=range(QUADRANTS)):
             for q in quadrants:
-                nc.sync.dma_start(plane[32 * q:32 * q + 4, :].bitcast(I32),
-                                  rows[first + 4 * q:first + 4 * q + 4, :].bitcast(I32))
+                nc.sync.dma_start(plane[q:P:32, :].bitcast(I32), rows[first + q:first + ROWS:4, :].bitcast(I32))
 
         def reorder_w4(dst, src):
             nc.vector.tensor_copy(dst.rearrange("p (b t m) -> p b t m", b=2, t=PACK),
@@ -140,33 +139,33 @@ def tile_list_map_change_gap_kernel(tc, tab_words, tab_scales, tab2_words, tab2_
         v2_w = {}
         for h in range(2):
             v2_w[0, h] = gather_half(own("v2_w0%d" % h, [P, HALF], U16), tab2_w[0], list2, h)
-        load_tw(0)
-        cast_w2(0, 1, nc.vector.tensor_copy, placed(area_f, "w2_bf01", [P, PACK * PASS], BF16))
-        load_tw(1)
-        quantise_w2(0, 1)
-        for h in range(2):
-            v2_w[1, h] = gather_half(placed(area_f + KB * h, "v2_w1%d" % h, [P, HALF], U16), tab2_w[1], list2, h)
-        w8_w = placed(area_c, "w8_w", [P, 2 * N], U32)
+        w8_w = placed(area_a, "w8_w", [P, 2 * N], U32)
         nc.sync.dma_start(w8_w[:].bitcast(I32).rearrange("p (b c) -> p b c", b=2),
                           w8_words.rearrange("b p c i -> p b (c i)").bitcast(I32))
-        w8_sc = placed(area_c + 4 * KB, "w8_sc", [P, N], U8)
+        w8_sc = placed(area_a + 4 * KB, "w8_sc", [P, N], U8)
         nc.vector.memset(w8_sc[:].bitcast(I32), 0)
         for q in range(QUADRANTS):
             nc.sync.dma_start(w8_sc[32 * q:32 * q + 8, :].bitcast(I32), w8_scales[:, 4 * q:4 * q + 4, :].bitcast(I32))
+        cast_w2(0, 1, nc.vector.tensor_copy, placed(area_f, "w2_bf01", [P, PACK * PASS], BF16))
+        load_tw(0)
+        quantise_w2(0, 1)
+        for h in range(2):
+            v2_w[1, h] = gather_half(placed(area_f + KB * h, "v2_w1%d" % h, [P, HALF], U16), tab2_w[1], list2, h)
+        load_tw(1)
 
-        scan_sb, diff, gap, gap_codes, gap_sc, weighted = {}, {}, {}, {}, {}, {}
+        scan_sb, diff, gap, gap_codes, gap_sc, y_ps, weighted = {}, {}, {}, {}, {}, {}, {}
 
         def bank(index, name):
             return psum.tile([P, HALF], F32, name=name, tag="bank%d" % index, bufs=1)
 
         shared_scans = {(0, 0, 2): area_e, (0, 0, 3): area_e + 4 * KB, (0, 1, 0): area_e + 8 * KB,
-                        (0, 1, 2): area_e + 10 * KB, (1, 1, 2): area_e + 12 * KB}
-        old_banks = {(0, 0): (4, 5, 6, 7), (0, 1): (0, 1, 2, 3), (1, 0): (4, 5, 6, 7), (1, 1): (5, 6, 7, 5)}
-        y_banks = ((0, 1, 2, 3), (4, 6, 7, 5))
+                        (0, 1, 1): area_e + 10 * KB, (1, 1, 1): area_e + 12 * KB}
+        old_banks = {(0, 0): (5, 6, 7, 1), (0, 1): (2, 3, 4, 0), (1, 0): (5, 6, 7, 1), (1, 1): (6, 7, 1, 6)}
+        y_banks = ((2, 3, 4, 0), (5, 7, 1, 6))
 
         def scan_block(b, h):
             for t in range(PACK):
-                acc = bank(t, "scan_ps")
+                acc = bank((PACK * (2 * h + b) + t) % 5, "scan_ps")
                 cols = slice(PASS * b + P * t, PASS * b + P * (t + 1))
                 nc.tensor.matmul_mx(out=acc[:], lhsT=w4_w[:, cols].bitcast(FP4X4),
                                     lhsT_scale=scan_planes[:, S + cols.start:S + cols.stop],
@@ -204,16 +203,18 @@ def tile_list_map_change_gap_kernel(tc, tab_words, tab_scales, tab2_words, tab2_
             gap_sc[b, h] = own("gap_sc%d%d" % (b, h), [P, HALF], U8)
             nc.vector.quantize_mx(out=gap_codes[b, h][:].bitcast(FP8X4), scales=gap_sc[b, h][:], in_=gap[b, h][:])
 
+        def y_pass(h, nt, b):
+            if b == 0:
+                y_ps[h, nt] = bank(y_banks[h][nt], "y_ps")
+            nc.tensor.matmul_mx(out=y_ps[h, nt][:], lhsT=w8_w[:, N * b + P * nt:N * b + P * (nt + 1)].bitcast(FP8X4),
+                                lhsT_scale=w8_sc[4 * b:P, P * nt:P * (nt + 1)],
+                                rhs=gap_codes[b, h][:].bitcast(FP8X4), rhs_scale=gap_sc[b, h][:],
+                                start=(b == 0), stop=(b == 1))
+
         def weigh(h, nt):
-            acc = bank(y_banks[h][nt], "y_ps")
-            for b in range(2):
-                nc.tensor.matmul_mx(out=acc[:], lhsT=w8_w[:, N * b + P * nt:N * b + P * (nt + 1)].bitcast(FP8X4),
-                                    lhsT_scale=w8_sc[4 * b:P, P * nt:P * (nt + 1)],
-                                    rhs=gap_codes[b, h][:].bitcast(FP8X4), rhs_scale=gap_sc[b, h][:],
-                                    start=(b == 0), stop=(b == 1))
             weighted[h, nt] = own("weighted%d%d" % (h, nt), [P, HALF], F32)
-            nc.vector.tensor_tensor(weighted[h, nt][:], acc[:], tw_sb[nt // 2][:, nt % 2, h * HALF:(h + 1) * HALF],
-                                    ALU.mult)
+            nc.vector.tensor_tensor(weighted[h, nt][:], y_ps[h, nt][:],
+                                    tw_sb[nt // 2][:, nt % 2, h * HALF:(h + 1) * HALF], ALU.mult)
 
         def store(h, nt):
             res = own("res%d%d" % (h, nt), [P, HALF], F32)
@@ -224,31 +225,33 @@ def tile_list_map_change_gap_kernel(tc, tab_words, tab_scales, tab2_words, tab2_
             for b in range(2):
                 scan_block(b, h)
         old_block(0, 0)
-        w2_bf10 = placed(area_e, "w2_bf10", [P, PACK * PASS], BF16)
-        cast_w2(1, 0, nc.vector.tensor_copy, w2_bf10, slice(0, PACK // 2))
-        cast_w2(1, 0, nc.scalar.copy, w2_bf10, slice(PACK // 2, PACK))
-        cast_w2(1, 1, nc.scalar.copy, placed(area_e + 4 * KB, "w2_bf11", [P, PACK * PASS], BF16))
-        old_block(0, 1, range(1))
-        quantise_w2(1, 0)
-        old_block(0, 1, range(1, PACK - 1))
-        quantise_w2(1, 1)
-        old_block(0, 1, range(PACK - 1, PACK))
+        for a in range(2):
+            grouped = placed(area_e + 4 * KB * a, "w2_bf1%d" % a, [P, PACK * PASS], BF16)
+            cast_w2(1, a, nc.vector.tensor_copy, grouped, slice(0, PACK // 2))
+            cast_w2(1, a, nc.scalar.copy, grouped, slice(PACK // 2, PACK))
+            old_block(0, 1, range(a, a + 1))
+            quantise_w2(1, a)
+        old_block(0, 1, range(2, PACK))
         for h in range(2):
             magnitudes(0, h)
         old_block(1, 0)
         magnitudes(1, 0)
-        old_block(1, 1, range(PACK - 1))
+        old_block(1, 1, range(2))
         quantise_gap(0, 0)
-        old_block(1, 1, range(PACK - 1, PACK))
+        old_block(1, 1, range(2, PACK))
         magnitudes(1, 1)
         quantise_gap(1, 0)
         quantise_gap(0, 1)
+        for h, b in ((0, 0), (0, 1), (1, 0)):
+            for nt in range(N // P):
+                y_pass(h, nt, b)
         weigh(0, 0)
         weigh(0, 1)
         quantise_gap(1, 1)
         weigh(0, 2)
         weigh(0, 3)
         for nt in range(N // P):
+            y_pass(1, nt, 1)
             weigh(1, nt)
         for h in range(2):
             for nt in range(N // P):

@@ -60,11 +60,13 @@ def tile_list_map_change_gap_kernel(tc, tab_words, tab_scales, tab2_words, tab2_
             tw_sb[g] = placed((area_a + 8 * KB, area_c)[g], "tw%d" % g, [P, 2, S], F32)
             nc.sync.dma_start(tw_sb[g][:], tw[2 * P * g:2 * P * (g + 1), :].rearrange("(i p) s -> p i s", p=P))
 
-        def load_rows(tile, scales, clearing_engine):
+        def load_rows(tile, scales, first):
             rows = scales.rearrange("a q c -> (a q) c")
-            first = P - rows.shape[0]
-            nc.sync.dma_start(tile[first:P, :].bitcast(I32), rows.bitcast(I32))
-            clearing_engine.memset(tile[0:first, :].bitcast(I32), 0)
+            last = first + rows.shape[0]
+            nc.sync.dma_start(tile[first:last, :].bitcast(I32), rows.bitcast(I32))
+            nc.vector.memset(tile[0:first, :].bitcast(I32), 0)
+            if last < P:
+                nc.gpsimd.memset(tile[last:P, :].bitcast(I32), 0)
 
         def move_rows(plane, rows, first, quadrants=range(QUADRANTS)):
             for q in quadrants:
@@ -75,15 +77,15 @@ def tile_list_map_change_gap_kernel(tc, tab_words, tab_scales, tab2_words, tab2_
                                   src.rearrange("p (b m t) -> p b t m", b=2, t=PACK))
 
         w4_rows = own("w4_rows", [P, H], U8)
-        load_rows(w4_rows, w4_scales, nc.vector)
+        load_rows(w4_rows, w4_scales, P - ROWS)
         w4_raw = own("w4_raw", [P, H], U16)
         nc.sync.dma_start(w4_raw[:].bitcast(I32), w4_words[0].bitcast(I32))
         nc.sync.dma_start(list1[:], offs)
         tab_rows = own("tab_rows", [P, T], U8)
-        load_rows(tab_rows, tab_scales, nc.vector)
+        load_rows(tab_rows, tab_scales, P - ROWS)
         nc.sync.dma_start(list2[:], offs2)
         tab2_rows = placed(area_c, "tab2_rows", [P, T], U8)
-        load_rows(tab2_rows, tab2_scales, nc.vector)
+        load_rows(tab2_rows, tab2_scales, 2 * ROWS)
         load_w2(0, 0, own("w2_raw00", [P, PACK, PASS], F32))
         tab_w = placed(area_b, "tab_w", [P, T], U32)
         nc.sync.dma_start(tab_w[:].bitcast(I32), tab_words[0].rearrange("p t i -> p (t i)").bitcast(I32))
@@ -107,10 +109,10 @@ def tile_list_map_change_gap_kernel(tc, tab_words, tab_scales, tab2_words, tab2_
 
         v2_rows = own("v2_rows", [P, S], U8)
         nc.vector.tensor_copy(v2_rows[:], tab2_rows[:].indirect(list2[:]))
-        move_rows(v2_planes[0], v2_rows, P - 2 * ROWS, range(2))
+        move_rows(v2_planes[0], v2_rows, 2 * ROWS, range(2))
         load_tab2(1)
-        move_rows(v2_planes[0], v2_rows, P - 2 * ROWS, range(2, QUADRANTS))
-        move_rows(v2_planes[1], v2_rows, P - ROWS)
+        move_rows(v2_planes[0], v2_rows, 2 * ROWS, range(2, QUADRANTS))
+        move_rows(v2_planes[1], v2_rows, 3 * ROWS)
 
         w2_bf, w2_codes, w2_sc = {}, {}, {}
 

@@ -22,239 +22,280 @@ PASS = P * PACK
 QUADRANTS = 4
 ROWS = 16
 HALF = S // 2
+CHUNK = S // 4
 RUN = 4
 KB = 1024
 
 
 def tile_list_map_change_gap_kernel(tc, tab_words, tab_scales, tab2_words, tab2_scales, offs, offs2,
-                                              w4_words, w4_scales, w2, w8_words, w8_scales, tw, out):
+                                                 w4_words, w4_scales, w2, w8_words, w8_scales, tw, out):
     nc = tc.nc
     with ExitStack() as ctx:
         keep = ctx.enter_context(tc.tile_pool(name="keep", bufs=1))
         shared = ctx.enter_context(tc.tile_pool(name="shared", bufs=1))
         psum = ctx.enter_context(tc.psum_pool(name="psum", bufs=1))
 
-        def own(name, shape, dtype):
-            return keep.tile(shape, dtype, name=name, align_bytes=64)
+        def tile(name, shape, dtype, at=None):
+            if at is None:
+                return keep.tile(shape, dtype, name=name, align_bytes=64)
+            return shared.tile(shape, dtype, name=name, align_bytes=64, offset=at)
 
-        def placed(offset, name, shape, dtype):
-            return shared.tile(shape, dtype, name=name, align_bytes=64, offset=offset)
+        def bank(index, name):
+            return psum.tile([P, 2 * CHUNK], F32, name=name, tag="bank%d" % index, bufs=1)
 
-        area_a, area_b, area_c, area_d, area_e, area_f, area_g = (
-            0, 16 * KB, 32 * KB, 40 * KB, 44 * KB, 60 * KB, 64 * KB)
+        area_a, area_b, area_c, area_d, area_f, area_e = 0, 16 * KB, 32 * KB, 40 * KB, 44 * KB, 48 * KB
 
         list1 = keep.tile([P, S // 16], U16, name="list1")
         list2 = keep.tile([P, S // 16], U16, name="list2")
         w2_raw, tab2_w, tw_sb = {}, {}, {}
 
-        def load_w2(b, a, tile):
-            w2_raw[b, a] = tile
-            nc.sync.dma_start(
-                tile[:], w2[PASS * a:PASS * (a + 1), PASS * b:PASS * (b + 1)].rearrange("(p j) c -> p j c", j=PACK))
+        def load_w2(b, a, at):
+            w2_raw[b, a] = tile("w2_raw%d%d" % (b, a), [P, PACK, PASS], F32, at)
+            nc.sync.dma_start(w2_raw[b, a][:], w2[PASS * a:PASS * (a + 1), PASS * b:PASS * (b + 1)].rearrange(
+                "(p j) c -> p j c", j=PACK))
 
-        def load_tab2(a):
-            tab2_w[a] = placed((area_a, area_c)[a], "tab2_w%d" % a, [P, T], U16)
+        def load_tab2(a, at):
+            tab2_w[a] = tile("tab2_w%d" % a, [P, T], U16, at)
             nc.sync.dma_start(tab2_w[a][:].bitcast(I32), tab2_words[a].bitcast(I32))
 
-        def load_tw(g):
-            tw_sb[g] = placed((area_a + 8 * KB, area_c)[g], "tw%d" % g, [P, 2, S], F32)
+        def load_tw(g, at):
+            tw_sb[g] = tile("tw%d" % g, [P, 2, S], F32, at)
             nc.sync.dma_start(tw_sb[g][:], tw[2 * P * g:2 * P * (g + 1), :].rearrange("(i p) s -> p i s", p=P))
 
-        def load_rows(tile, scales, first):
+        def load_rows(rows_tile, scales, first):
             rows = scales.rearrange("a q c -> (a q) c")
             last = first + rows.shape[0]
-            nc.sync.dma_start(tile[first:last, :].bitcast(I32), rows.bitcast(I32))
-            nc.vector.memset(tile[0:first, :].bitcast(I32), 0)
+            nc.sync.dma_start(rows_tile[first:last, :].bitcast(I32), rows.bitcast(I32))
+            nc.vector.memset(rows_tile[0:first, :].bitcast(I32), 0)
             if last < P:
-                nc.gpsimd.memset(tile[last:P, :].bitcast(I32), 0)
+                nc.gpsimd.memset(rows_tile[last:P, :].bitcast(I32), 0)
 
-        def move_rows(plane, rows, first, quadrants=range(QUADRANTS)):
-            for q in quadrants:
-                nc.sync.dma_start(plane[q:P:32, :].bitcast(I32), rows[first + q:first + ROWS:4, :].bitcast(I32))
+        def move_rows(plane, rows, first, which=range(QUADRANTS)):
+            for r in which:
+                nc.sync.dma_start(plane[r:P:32, :].bitcast(I32), rows[first + r:first + ROWS:4, :].bitcast(I32))
 
-        def reorder_w4(dst, src):
+        def deal_w4(dst, src):
             nc.vector.tensor_copy(dst.rearrange("p (b t m) -> p b t m", b=2, t=PACK),
                                   src.rearrange("p (b m t) -> p b t m", b=2, t=PACK))
 
-        w4_rows = own("w4_rows", [P, H], U8)
+        w4_rows = tile("w4_rows", [P, H], U8)
         load_rows(w4_rows, w4_scales, P - ROWS)
-        w4_raw = own("w4_raw", [P, H], U16)
+        w4_raw = tile("w4_raw", [P, H], U16)
         nc.sync.dma_start(w4_raw[:].bitcast(I32), w4_words[0].bitcast(I32))
         nc.sync.dma_start(list1[:], offs)
-        tab_rows = own("tab_rows", [P, T], U8)
+        tab_rows = tile("tab_rows", [P, T], U8)
         load_rows(tab_rows, tab_scales, P - ROWS)
         nc.sync.dma_start(list2[:], offs2)
-        tab2_rows = placed(area_c, "tab2_rows", [P, T], U8)
+        tab2_rows = tile("tab2_rows", [P, T], U8, area_c)
         load_rows(tab2_rows, tab2_scales, 2 * ROWS)
-        load_w2(0, 0, own("w2_raw00", [P, PACK, PASS], F32))
-        tab_w = placed(area_b, "tab_w", [P, T], U32)
+        load_w2(0, 0, None)
+        tab_w = tile("tab_w", [P, T], U32, area_b)
         nc.sync.dma_start(tab_w[:].bitcast(I32), tab_words[0].rearrange("p t i -> p (t i)").bitcast(I32))
 
-        scan_planes = own("scan_planes", [P, S + H], U8)
+        scan_planes = tile("scan_planes", [P, S + H], U8)
         nc.vector.memset(scan_planes[:].bitcast(I32), 0)
-        v2_planes = [own("v2_plane%d" % a, [P, S], U8) for a in range(2)]
+        v2_planes = [tile("v2_plane%d" % a, [P, S], U8) for a in range(2)]
         for plane in v2_planes:
             nc.vector.memset(plane[:].bitcast(I32), 0)
 
-        scan_rows = own("scan_rows", [P, S + H], U8)
-        reorder_w4(scan_rows[:, S:S + H], w4_rows[:])
-        w4_w = own("w4_w", [P, H], U16)
-        reorder_w4(w4_w[:], w4_raw[:])
-        v_rows = placed(area_a + 8 * KB - S // 2, "v_rows", [P, S], U8)
+        scan_rows = tile("scan_rows", [P, S + H], U8)
+        deal_w4(scan_rows[:, S:S + H], w4_rows[:])
+        w4_w = tile("w4_w", [P, H], U16)
+        deal_w4(w4_w[:], w4_raw[:])
+        v_rows = tile("v_rows", [P, S], U8, area_a + 8 * KB - S // 2)
         nc.vector.tensor_copy(v_rows[:], tab_rows[:].indirect(list1[:]))
         nc.vector.tensor_copy(scan_rows[:, 0:S].bitcast(I32), v_rows[:].bitcast(I32))
         move_rows(scan_planes, scan_rows, P - ROWS)
-        load_tab2(0)
-        load_w2(0, 1, placed(area_a + 8 * KB, "w2_raw01", [P, PACK, PASS], F32))
+        load_tab2(0, area_a)
+        load_w2(0, 1, area_a + 8 * KB)
 
-        v2_rows = own("v2_rows", [P, S], U8)
+        v2_rows = tile("v2_rows", [P, S], U8)
         nc.vector.tensor_copy(v2_rows[:], tab2_rows[:].indirect(list2[:]))
         move_rows(v2_planes[0], v2_rows, 2 * ROWS, range(2))
-        load_tab2(1)
+        load_tab2(1, area_c)
         move_rows(v2_planes[0], v2_rows, 2 * ROWS, range(2, QUADRANTS))
         move_rows(v2_planes[1], v2_rows, 3 * ROWS)
 
         w2_bf, w2_codes, w2_sc = {}, {}, {}
 
-        def cast_w2(b, a, cast, tile, part=slice(0, PACK)):
-            w2_bf[b, a] = tile
-            cast(tile[:, PASS * part.start:PASS * part.stop].rearrange("p (t m j) -> p m t j", m=P, j=PACK),
+        def round_on_gpsimd(dst, src):
+            nc.gpsimd.tensor_scalar(dst, src, 1.0, 0.0, ALU.mult, ALU.add)
+
+        def round_w2(b, a, cast, at, part=slice(0, PACK)):
+            if (b, a) not in w2_bf:
+                w2_bf[b, a] = tile("w2_bf%d%d" % (b, a), [P, PACK * PASS], BF16, at)
+            cast(w2_bf[b, a][:, PASS * part.start:PASS * part.stop].rearrange("p (t m j) -> p m t j", m=P, j=PACK),
                  w2_raw[b, a][:].rearrange("p j (m t) -> p m t j", t=PACK)[:, :, part, :])
 
-        def quantise_w2(b, a):
-            name = "w2_codes%d%d" % (b, a)
-            w2_codes[b, a] = placed(area_e + (8 + 2 * a) * KB, name, [P, PASS], U32) if b == 1 else own(
-                name, [P, PASS], U32)
-            w2_sc[b, a] = own("w2_sc%d%d" % (b, a), [P, PASS], U8)
+        def quantise_w2(b, a, at=None):
+            w2_codes[b, a] = tile("w2_codes%d%d" % (b, a), [P, PASS], U32, at)
+            w2_sc[b, a] = tile("w2_sc%d%d" % (b, a), [P, PASS], U8)
             nc.vector.quantize_mx(out=w2_codes[b, a][:].bitcast(FP8X4), scales=w2_sc[b, a][:], in_=w2_bf[b, a][:])
 
         def gather_half(picked, window, offsets, h):
             nc.vector.tensor_copy(picked[:], window[:].indirect(offsets[:, h * HALF // 16:(h + 1) * HALF // 16]))
             return picked
 
-        cast_w2(0, 0, nc.scalar.copy, placed(area_d, "w2_bf00", [P, PACK * PASS], BF16))
+        round_w2(0, 0, nc.scalar.copy, area_d)
         quantise_w2(0, 0)
-        v_w = [gather_half(placed(area_d + 2 * KB * h, "v_w%d" % h, [P, HALF], U32), tab_w, list1, h)
+        v_w = [gather_half(tile("v_w%d" % h, [P, HALF], U32, area_d + 2 * KB * h), tab_w, list1, h)
                for h in range(2)]
         for a in range(2):
-            load_w2(1, a, placed(area_b + 8 * KB * a, "w2_raw1%d" % a, [P, PACK, PASS], F32))
+            load_w2(1, a, area_b + 8 * KB * a)
         v2_w = {}
         for h in range(2):
-            v2_w[0, h] = gather_half(own("v2_w0%d" % h, [P, HALF], U16), tab2_w[0], list2, h)
-        w8_w = placed(area_a, "w8_w", [P, 2 * N], U32)
+            v2_w[0, h] = gather_half(tile("v2_w0%d" % h, [P, HALF], U16), tab2_w[0], list2, h)
+        w8_w = tile("w8_w", [P, 2 * N], U32, area_a)
         nc.sync.dma_start(w8_w[:].bitcast(I32).rearrange("p (b c) -> p b c", b=2),
                           w8_words.rearrange("b p c i -> p b (c i)").bitcast(I32))
-        w8_sc = placed(area_a + 4 * KB, "w8_sc", [P, N], U8)
+        w8_sc = tile("w8_sc", [P, N], U8, area_a + 4 * KB)
         nc.vector.memset(w8_sc[:].bitcast(I32), 0)
         for q in range(QUADRANTS):
             nc.sync.dma_start(w8_sc[32 * q:32 * q + 8, :].bitcast(I32), w8_scales[:, 4 * q:4 * q + 4, :].bitcast(I32))
-        cast_w2(0, 1, nc.vector.tensor_copy, placed(area_f, "w2_bf01", [P, PACK * PASS], BF16))
-        load_tw(0)
+        round_w2(0, 1, nc.vector.tensor_copy, area_f)
+        load_tw(0, area_a + 8 * KB)
         quantise_w2(0, 1)
         for h in range(2):
-            v2_w[1, h] = gather_half(placed(area_f + KB * h, "v2_w1%d" % h, [P, HALF], U16), tab2_w[1], list2, h)
-        load_tw(1)
+            v2_w[1, h] = gather_half(tile("v2_w1%d" % h, [P, HALF], U16, area_f + KB * h), tab2_w[1], list2, h)
+        load_tw(1, area_c)
 
         scan_sb, diff, gap, gap_codes, gap_sc, y_ps, weighted = {}, {}, {}, {}, {}, {}, {}
+        scan_at = {(0, 1, 1): area_e, (0, 3, 0): area_e + 4 * KB, (0, 3, 1): area_e + 6 * KB}
+        old_banks = ((5, 6, 7, 1, 2, 3, 4, 2), (5, 6, 7, 1, 0, 3, 4, 2))
 
-        def bank(index, name):
-            return psum.tile([P, HALF], F32, name=name, tag="bank%d" % index, bufs=1)
+        def half_cols(c):
+            return slice(CHUNK * (c % 2), CHUNK * (c % 2 + 1))
 
-        shared_scans = {(0, 0, 2): area_e, (0, 0, 3): area_e + 4 * KB, (0, 1, 0): area_e + 8 * KB,
-                        (0, 1, 1): area_e + 10 * KB, (1, 1, 1): area_e + 12 * KB}
-        old_banks = {(0, 0): (5, 6, 7, 1), (0, 1): (2, 3, 4, 0), (1, 0): (5, 6, 7, 1), (1, 1): (6, 7, 1, 6)}
-        y_banks = ((2, 3, 4, 0), (5, 7, 1, 6))
+        def list_cols(c):
+            return slice(CHUNK * c, CHUNK * (c + 1))
 
-        def scan_block(b, h):
-            for t in range(PACK):
-                acc = bank((PACK * (2 * h + b) + t) % 5, "scan_ps")
-                cols = slice(PASS * b + P * t, PASS * b + P * (t + 1))
-                nc.tensor.matmul_mx(out=acc[:], lhsT=w4_w[:, cols].bitcast(FP4X4),
-                                    lhsT_scale=scan_planes[:, S + cols.start:S + cols.stop],
-                                    rhs=v_w[h][:].bitcast(FP8X4), rhs_scale=scan_planes[:, h * HALF:(h + 1) * HALF],
-                                    start=True, stop=True)
-                name = "scan%d%d%d" % (b, h, t)
-                scan_sb[b, h, t] = placed(shared_scans[b, h, t], name, [P, HALF], F32) if (b, h, t) in shared_scans else own(
-                    name, [P, HALF], F32)
-                nc.scalar.copy(scan_sb[b, h, t][:], acc[:])
+        def scan_bank(b, c, g):
+            acc = bank((8 * b + 2 * c + g) % 5, "scan_ps")
+            for i in range(2):
+                col = PASS * b + P * (2 * g + i)
+                nc.tensor.matmul_mx(out=acc[:, list_cols(i)], lhsT=w4_w[:, col:col + P].bitcast(FP4X4),
+                                    lhsT_scale=scan_planes[:, S + col:S + col + P],
+                                    rhs=v_w[c // 2][:, half_cols(c)].bitcast(FP8X4),
+                                    rhs_scale=scan_planes[:, list_cols(c)], start=True, stop=True)
+            scan_sb[b, c, g] = tile("scan%d%d%d" % (b, c, g), [P, 2 * CHUNK], F32, scan_at.get((b, c, g)))
+            nc.scalar.copy(scan_sb[b, c, g][:], acc[:])
 
-        def old_block(b, h, rows=range(PACK)):
-            if (b, h) not in diff:
-                diff[b, h] = own("diff%d%d" % (b, h), [P, PACK, HALF], BF16)
-            for t in rows:
-                acc = bank(old_banks[b, h][t], "old_ps")
-                cols = slice(P * t, P * (t + 1))
-                for a in (b ^ 1, b):
-                    nc.tensor.matmul_mx(out=acc[:], lhsT=w2_codes[b, a][:, cols].bitcast(FP8X4),
-                                        lhsT_scale=w2_sc[b, a][:, cols], rhs=v2_w[a, h][:].bitcast(FP4X4),
-                                        rhs_scale=v2_planes[a][:, h * HALF:(h + 1) * HALF],
-                                        start=(a != b), stop=(a == b))
-                nc.vector.tensor_tensor(diff[b, h][:, t, :], acc[:], scan_sb[b, h, t][:], ALU.subtract)
+        def old_bank(b, c, g, first_pass):
+            if g == 0:
+                diff[b, c] = tile("diff%d%d" % (b, c), [P, PACK * CHUNK], BF16)
+            acc = bank(old_banks[b][2 * c + g], "old_ps")
+            for step, (a, i) in enumerate((a, i) for a in (first_pass, 1 - first_pass) for i in range(2)):
+                cols = slice(P * (2 * g + i), P * (2 * g + i + 1))
+                nc.tensor.matmul_mx(out=acc[:, list_cols(i)], lhsT=w2_codes[b, a][:, cols].bitcast(FP8X4),
+                                    lhsT_scale=w2_sc[b, a][:, cols],
+                                    rhs=v2_w[a, c // 2][:, half_cols(c)].bitcast(FP4X4),
+                                    rhs_scale=v2_planes[a][:, list_cols(c)], start=(step == 0), stop=(step == 3))
+            nc.vector.tensor_tensor(diff[b, c][:, 2 * CHUNK * g:2 * CHUNK * (g + 1)], acc[:], scan_sb[b, c, g][:],
+                                    ALU.subtract)
 
-        def magnitudes(b, h):
-            name = "gap%d%d" % (b, h)
-            gap[b, h] = placed((area_b + 8 * KB, area_g)[b], name, [P, HALF * PACK], BF16) if h == 0 else own(
-                name, [P, HALF * PACK], BF16)
-            nc.scalar.activation(gap[b, h][:].rearrange("p (c i t) -> p c t i", i=RUN, t=PACK),
-                                 diff[b, h][:].rearrange("p t (c i) -> p c t i", i=RUN), ABS)
+        def old_chunk(b, c, first_pass=1):
+            for g in range(2):
+                old_bank(b, c, g, first_pass)
 
-        def quantise_gap(b, h):
-            name = "gap_codes%d%d" % (b, h)
-            gap_codes[b, h] = placed((area_e + 12 * KB, area_g)[h], name, [P, HALF], U32) if b == 0 else own(
-                name, [P, HALF], U32)
-            gap_sc[b, h] = own("gap_sc%d%d" % (b, h), [P, HALF], U8)
-            nc.vector.quantize_mx(out=gap_codes[b, h][:].bitcast(FP8X4), scales=gap_sc[b, h][:], in_=gap[b, h][:])
+        def magnitudes(b, c, at=None):
+            if b == 1:
+                gap[b, c] = tile("gap1%d" % c, [P, CHUNK * PACK], BF16, at)
+                dst = gap[b, c][:]
+            else:
+                if c % 2 == 0:
+                    gap[b, c // 2] = tile("gap0%d" % (c // 2), [P, HALF * PACK], BF16, at)
+                dst = gap[b, c // 2][:, PACK * CHUNK * (c % 2):PACK * CHUNK * (c % 2 + 1)]
+            nc.scalar.activation(dst.rearrange("p (s i t) -> p s t i", i=RUN, t=PACK),
+                                 diff[b, c][:].rearrange("p (t s i) -> p s t i", t=PACK, i=RUN), ABS)
 
-        def y_pass(h, nt, b):
-            if b == 0:
-                y_ps[h, nt] = bank(y_banks[h][nt], "y_ps")
-            nc.tensor.matmul_mx(out=y_ps[h, nt][:], lhsT=w8_w[:, N * b + P * nt:N * b + P * (nt + 1)].bitcast(FP8X4),
-                                lhsT_scale=w8_sc[4 * b:P, P * nt:P * (nt + 1)],
-                                rhs=gap_codes[b, h][:].bitcast(FP8X4), rhs_scale=gap_sc[b, h][:],
-                                start=(b == 0), stop=(b == 1))
+        def quantise_gap(b, part, at=None):
+            width = (HALF, CHUNK)[b]
+            gap_codes[b, part] = tile("gap_codes%d%d" % (b, part), [P, width], U32, at)
+            gap_sc[b, part] = tile("gap_sc%d%d" % (b, part), [P, width], U8)
+            nc.vector.quantize_mx(out=gap_codes[b, part][:].bitcast(FP8X4), scales=gap_sc[b, part][:],
+                                  in_=gap[b, part][:])
 
-        def weigh(h, nt):
-            weighted[h, nt] = own("weighted%d%d" % (h, nt), [P, HALF], F32)
-            nc.vector.tensor_tensor(weighted[h, nt][:], y_ps[h, nt][:],
-                                    tw_sb[nt // 2][:, nt % 2, h * HALF:(h + 1) * HALF], ALU.mult)
+        def y_passes(c, b):
+            part, cols = ((c // 2, half_cols(c)), (c, slice(0, CHUNK)))[b]
+            for g in range(2):
+                if b == 0:
+                    y_ps[c, g] = bank(old_banks[1][2 * c + g], "y_ps")
+                for i in range(2):
+                    col = P * (2 * g + i)
+                    nc.tensor.matmul_mx(out=y_ps[c, g][:, list_cols(i)],
+                                        lhsT=w8_w[:, N * b + col:N * b + col + P].bitcast(FP8X4),
+                                        lhsT_scale=w8_sc[4 * b:P, col:col + P],
+                                        rhs=gap_codes[b, part][:, cols].bitcast(FP8X4),
+                                        rhs_scale=gap_sc[b, part][:, cols],
+                                        start=(b == 0 and i == 0), stop=(b == 1 and i == 1))
 
-        def store(h, nt):
-            res = own("res%d%d" % (h, nt), [P, HALF], F32)
-            nc.scalar.activation(res[:], weighted[h, nt][:], ABS)
-            nc.sync.dma_start(out[P * nt:P * (nt + 1), HALF * h:HALF * (h + 1)], res[:])
+        def pair_view(ap):
+            return ap.rearrange("p (i s) -> p i s", i=2)
 
-        for h in range(2):
-            for b in range(2):
-                scan_block(b, h)
-        old_block(0, 0)
-        for a in range(2):
-            grouped = placed(area_e + 4 * KB * a, "w2_bf1%d" % a, [P, PACK * PASS], BF16)
-            cast_w2(1, a, nc.vector.tensor_copy, grouped, slice(0, PACK // 2))
-            cast_w2(1, a, nc.scalar.copy, grouped, slice(PACK // 2, PACK))
-            old_block(0, 1, range(a, a + 1))
-            quantise_w2(1, a)
-        old_block(0, 1, range(2, PACK))
-        for h in range(2):
-            magnitudes(0, h)
-        old_block(1, 0)
+        def store(c, g, res):
+            nc.sync.dma_start(out[2 * P * g:2 * P * (g + 1), list_cols(c)].rearrange("(i p) s -> p i s", p=P),
+                              pair_view(res[:]))
+
+        def weigh_then_magnitude(c, g):
+            weighted = tile("weighted%d%d" % (c, g), [P, 2 * CHUNK], F32)
+            nc.vector.tensor_tensor(pair_view(weighted[:]), pair_view(y_ps[c, g][:]), tw_sb[g][:, :, list_cols(c)],
+                                    ALU.mult)
+            res = tile("res%d%d" % (c, g), [P, 2 * CHUNK], F32)
+            nc.scalar.activation(res[:], weighted[:], ABS)
+            store(c, g, res)
+
+        def magnitude_then_weigh(c, g, engine):
+            size = tile("size%d%d" % (c, g), [P, 2 * CHUNK], F32)
+            nc.scalar.activation(size[:], y_ps[c, g][:], ABS)
+            res = tile("res%d%d" % (c, g), [P, 2 * CHUNK], F32)
+            engine.tensor_tensor(pair_view(res[:]), pair_view(size[:]), tw_sb[g][:, :, list_cols(c)], ALU.mult)
+            store(c, g, res)
+
+        for b in range(2):
+            for c in range(4):
+                for g in range(2):
+                    scan_bank(b, c, g)
+        round_w2(1, 0, round_on_gpsimd, None)
+        old_chunk(0, 0)
+        magnitudes(0, 0)
+        old_chunk(0, 1)
+        round_w2(1, 1, nc.scalar.copy, area_e, slice(0, PACK - 1))
+        round_w2(1, 1, round_on_gpsimd, area_e, slice(PACK - 1, PACK))
+        magnitudes(0, 1)
+        old_chunk(0, 2)
+        magnitudes(0, 2, area_b + 8 * KB)
+        old_bank(0, 3, 0, 1)
+        quantise_w2(1, 0, area_e + 4 * KB)
+        old_bank(0, 3, 1, 1)
+        magnitudes(0, 3)
+        quantise_w2(1, 1, area_e + 6 * KB)
+        quantise_gap(0, 0, area_e + 2 * KB)
+        old_chunk(1, 0, 0)
         magnitudes(1, 0)
-        old_block(1, 1, range(2))
-        quantise_gap(0, 0)
-        old_block(1, 1, range(2, PACK))
+        old_chunk(1, 1)
         magnitudes(1, 1)
         quantise_gap(1, 0)
-        quantise_gap(0, 1)
-        for h, b in ((0, 0), (0, 1), (1, 0)):
-            for nt in range(N // P):
-                y_pass(h, nt, b)
-        weigh(0, 0)
-        weigh(0, 1)
+        old_chunk(1, 2)
+        magnitudes(1, 2)
+        y_passes(0, 0)
+        y_passes(0, 1)
         quantise_gap(1, 1)
-        weigh(0, 2)
-        weigh(0, 3)
-        for nt in range(N // P):
-            y_pass(1, nt, 1)
-            weigh(1, nt)
-        for h in range(2):
-            for nt in range(N // P):
-                store(h, nt)
+        weigh_then_magnitude(0, 0)
+        weigh_then_magnitude(0, 1)
+        old_chunk(1, 3)
+        magnitudes(1, 3)
+        y_passes(1, 0)
+        y_passes(1, 1)
+        quantise_gap(0, 1)
+        quantise_gap(1, 2)
+        y_passes(2, 0)
+        y_passes(2, 1)
+        weigh_then_magnitude(1, 0)
+        weigh_then_magnitude(1, 1)
+        quantise_gap(1, 3)
+        y_passes(3, 0)
+        y_passes(3, 1)
+        weigh_then_magnitude(2, 0)
+        weigh_then_magnitude(2, 1)
+        weigh_then_magnitude(3, 0)
+        magnitude_then_weigh(3, 1, nc.vector)

@@ -159,9 +159,11 @@ def tile_list_map_change_gap_kernel(tc, tab_words, tab_scales, tab2_words, tab2_
             v2_w[1, h] = gather_half(tile("v2_w1%d" % h, [P, HALF], U16, area_f + KB * h), tab2_w[1], list2, h)
         load_tw(1, area_c)
 
-        scan_sb, diff, gap, gap_codes, gap_sc, y_ps, weighted = {}, {}, {}, {}, {}, {}, {}
+        scan_sb, diff, gap, gap_codes, gap_sc, y_ps, halfway = {}, {}, {}, {}, {}, {}, {}
         scan_at = {(0, 1, 1): area_e, (0, 3, 0): area_e + 4 * KB, (0, 3, 1): area_e + 6 * KB}
         old_banks = ((5, 6, 7, 1, 2, 3, 4, 2), (5, 6, 7, 1, 0, 3, 4, 2))
+
+        y_banks = (4, 2, 5, 6, 7, 1, 0, 3)
 
         def half_cols(c):
             return slice(CHUNK * (c % 2), CHUNK * (c % 2 + 1))
@@ -180,9 +182,9 @@ def tile_list_map_change_gap_kernel(tc, tab_words, tab_scales, tab2_words, tab2_
             scan_sb[b, c, g] = tile("scan%d%d%d" % (b, c, g), [P, 2 * CHUNK], F32, scan_at.get((b, c, g)))
             nc.scalar.copy(scan_sb[b, c, g][:], acc[:])
 
-        def old_bank(b, c, g, first_pass):
+        def old_bank(b, c, g, first_pass, at=None):
             if g == 0:
-                diff[b, c] = tile("diff%d%d" % (b, c), [P, PACK * CHUNK], BF16)
+                diff[b, c] = tile("diff%d%d" % (b, c), [P, PACK * CHUNK], BF16, at)
             acc = bank(old_banks[b][2 * c + g], "old_ps")
             for step, (a, i) in enumerate((a, i) for a in (first_pass, 1 - first_pass) for i in range(2)):
                 cols = slice(P * (2 * g + i), P * (2 * g + i + 1))
@@ -193,9 +195,9 @@ def tile_list_map_change_gap_kernel(tc, tab_words, tab_scales, tab2_words, tab2_
             nc.vector.tensor_tensor(diff[b, c][:, 2 * CHUNK * g:2 * CHUNK * (g + 1)], acc[:], scan_sb[b, c, g][:],
                                     ALU.subtract)
 
-        def old_chunk(b, c, first_pass=1):
+        def old_chunk(b, c, first_pass=1, at=None):
             for g in range(2):
-                old_bank(b, c, g, first_pass)
+                old_bank(b, c, g, first_pass, at)
 
         def magnitudes(b, c, at=None):
             if b == 1:
@@ -219,7 +221,7 @@ def tile_list_map_change_gap_kernel(tc, tab_words, tab_scales, tab2_words, tab2_
             part, cols = ((c // 2, half_cols(c)), (c, slice(0, CHUNK)))[b]
             for g in range(2):
                 if b == 0:
-                    y_ps[c, g] = bank(old_banks[1][2 * c + g], "y_ps")
+                    y_ps[c, g] = bank(y_banks[2 * c + g], "y_ps")
                 for i in range(2):
                     col = P * (2 * g + i)
                     nc.tensor.matmul_mx(out=y_ps[c, g][:, list_cols(i)],
@@ -236,19 +238,25 @@ def tile_list_map_change_gap_kernel(tc, tab_words, tab_scales, tab2_words, tab2_
             nc.sync.dma_start(out[2 * P * g:2 * P * (g + 1), list_cols(c)].rearrange("(i p) s -> p i s", p=P),
                               pair_view(res[:]))
 
-        def weigh_then_magnitude(c, g):
-            weighted = tile("weighted%d%d" % (c, g), [P, 2 * CHUNK], F32)
-            nc.vector.tensor_tensor(pair_view(weighted[:]), pair_view(y_ps[c, g][:]), tw_sb[g][:, :, list_cols(c)],
-                                    ALU.mult)
+        def tw_cols(c, g):
+            return tw_sb[g][:, :, list_cols(c)]
+
+        def weigh_bank(c, g):
+            halfway[c, g] = tile("weighted%d%d" % (c, g), [P, 2 * CHUNK], F32)
+            nc.vector.tensor_tensor(pair_view(halfway[c, g][:]), pair_view(y_ps[c, g][:]), tw_cols(c, g), ALU.mult)
+
+        def magnitude_and_store(c, g):
             res = tile("res%d%d" % (c, g), [P, 2 * CHUNK], F32)
-            nc.scalar.activation(res[:], weighted[:], ABS)
+            nc.scalar.activation(res[:], halfway[c, g][:], ABS)
             store(c, g, res)
 
-        def magnitude_then_weigh(c, g, engine):
-            size = tile("size%d%d" % (c, g), [P, 2 * CHUNK], F32)
-            nc.scalar.activation(size[:], y_ps[c, g][:], ABS)
-            res = tile("res%d%d" % (c, g), [P, 2 * CHUNK], F32)
-            engine.tensor_tensor(pair_view(res[:]), pair_view(size[:]), tw_sb[g][:, :, list_cols(c)], ALU.mult)
+        def magnitude_of_bank(c, g, at=None):
+            halfway[c, g] = tile("size%d%d" % (c, g), [P, 2 * CHUNK], F32, at)
+            nc.scalar.activation(halfway[c, g][:], y_ps[c, g][:], ABS)
+
+        def weigh_and_store(c, g, engine, at=None):
+            res = tile("res%d%d" % (c, g), [P, 2 * CHUNK], F32, at)
+            engine.tensor_tensor(pair_view(res[:]), pair_view(halfway[c, g][:]), tw_cols(c, g), ALU.mult)
             store(c, g, res)
 
         for b in range(2):
@@ -259,8 +267,8 @@ def tile_list_map_change_gap_kernel(tc, tab_words, tab_scales, tab2_words, tab2_
         old_chunk(0, 0)
         magnitudes(0, 0)
         old_chunk(0, 1)
-        round_w2(1, 1, nc.scalar.copy, area_e, slice(0, PACK - 1))
-        round_w2(1, 1, round_on_gpsimd, area_e, slice(PACK - 1, PACK))
+        round_w2(1, 1, nc.scalar.copy, area_e, slice(0, PACK // 2))
+        round_w2(1, 1, round_on_gpsimd, area_e, slice(PACK // 2, PACK))
         magnitudes(0, 1)
         old_chunk(0, 2)
         magnitudes(0, 2, area_b + 8 * KB)
@@ -273,29 +281,37 @@ def tile_list_map_change_gap_kernel(tc, tab_words, tab_scales, tab2_words, tab2_
         old_chunk(1, 0, 0)
         magnitudes(1, 0)
         old_chunk(1, 1)
-        magnitudes(1, 1)
-        quantise_gap(1, 0)
-        old_chunk(1, 2)
-        magnitudes(1, 2)
+        magnitudes(1, 1, area_e + 8 * KB)
         y_passes(0, 0)
+        quantise_gap(1, 0)
         y_passes(0, 1)
+        quantise_gap(0, 1)
         quantise_gap(1, 1)
-        weigh_then_magnitude(0, 0)
-        weigh_then_magnitude(0, 1)
-        old_chunk(1, 3)
-        magnitudes(1, 3)
+        old_chunk(1, 2, 1, area_e + 8 * KB)
         y_passes(1, 0)
         y_passes(1, 1)
-        quantise_gap(0, 1)
-        quantise_gap(1, 2)
+        magnitude_of_bank(0, 0)
+        weigh_and_store(0, 0, nc.gpsimd)
+        magnitude_of_bank(0, 1, area_e + 10 * KB)
+        weigh_and_store(0, 1, nc.gpsimd)
+        magnitude_of_bank(1, 0)
+        magnitudes(1, 2)
+        old_chunk(1, 3)
+        magnitudes(1, 3)
+        weigh_bank(1, 1)
+        quantise_gap(1, 2, area_e + 10 * KB)
         y_passes(2, 0)
         y_passes(2, 1)
-        weigh_then_magnitude(1, 0)
-        weigh_then_magnitude(1, 1)
+        weigh_and_store(1, 0, nc.vector, area_e + 11 * KB)
         quantise_gap(1, 3)
         y_passes(3, 0)
         y_passes(3, 1)
-        weigh_then_magnitude(2, 0)
-        weigh_then_magnitude(2, 1)
-        weigh_then_magnitude(3, 0)
-        magnitude_then_weigh(3, 1, nc.vector)
+        magnitude_and_store(1, 1)
+        weigh_bank(2, 0)
+        magnitude_of_bank(2, 1)
+        weigh_bank(3, 1)
+        magnitude_and_store(2, 0)
+        weigh_and_store(2, 1, nc.vector)
+        magnitude_of_bank(3, 0)
+        weigh_and_store(3, 0, nc.vector)
+        magnitude_and_store(3, 1)

@@ -23,7 +23,6 @@ QUADRANTS = 4
 ROWS = 16
 HALF = S // 2
 CHUNK = S // 4
-RUN = 4
 KB = 1024
 
 
@@ -171,6 +170,9 @@ def tile_list_map_change_gap_kernel(tc, tab_words, tab_scales, tab2_words, tab2_
         def list_cols(c):
             return slice(CHUNK * c, CHUNK * (c + 1))
 
+        def woven(acc):
+            return acc[:].rearrange("p (i s) -> p s i", i=2)
+
         def scan_bank(b, c, g):
             acc = bank((8 * b + 2 * c + g) % 5, "scan_ps")
             for i in range(2):
@@ -180,7 +182,7 @@ def tile_list_map_change_gap_kernel(tc, tab_words, tab_scales, tab2_words, tab2_
                                     rhs=v_w[c // 2][:, half_cols(c)].bitcast(FP8X4),
                                     rhs_scale=scan_planes[:, list_cols(c)], start=True, stop=True)
             scan_sb[b, c, g] = tile("scan%d%d%d" % (b, c, g), [P, 2 * CHUNK], F32, scan_at.get((b, c, g)))
-            nc.scalar.copy(scan_sb[b, c, g][:], acc[:])
+            nc.scalar.copy(scan_sb[b, c, g][:].rearrange("p (s i) -> p s i", i=2), woven(acc))
 
         def old_bank(b, c, g, first_pass, at=None):
             if g == 0:
@@ -192,8 +194,8 @@ def tile_list_map_change_gap_kernel(tc, tab_words, tab_scales, tab2_words, tab2_
                                     lhsT_scale=w2_sc[b, a][:, cols],
                                     rhs=v2_w[a, c // 2][:, half_cols(c)].bitcast(FP4X4),
                                     rhs_scale=v2_planes[a][:, list_cols(c)], start=(step == 0), stop=(step == 3))
-            nc.vector.tensor_tensor(diff[b, c][:, 2 * CHUNK * g:2 * CHUNK * (g + 1)], acc[:], scan_sb[b, c, g][:],
-                                    ALU.subtract)
+            nc.vector.tensor_tensor(diff[b, c][:, 2 * CHUNK * g:2 * CHUNK * (g + 1)].rearrange("p (s i) -> p s i", i=2),
+                                    woven(acc), scan_sb[b, c, g][:].rearrange("p (s i) -> p s i", i=2), ALU.subtract)
 
         def old_chunk(b, c, first_pass=1, at=None):
             for g in range(2):
@@ -207,8 +209,8 @@ def tile_list_map_change_gap_kernel(tc, tab_words, tab_scales, tab2_words, tab2_
                 if c % 2 == 0:
                     gap[b, c // 2] = tile("gap0%d" % (c // 2), [P, HALF * PACK], BF16, at)
                 dst = gap[b, c // 2][:, PACK * CHUNK * (c % 2):PACK * CHUNK * (c % 2 + 1)]
-            nc.scalar.activation(dst.rearrange("p (s i t) -> p s t i", i=RUN, t=PACK),
-                                 diff[b, c][:].rearrange("p (t s i) -> p s t i", t=PACK, i=RUN), ABS)
+            nc.scalar.activation(dst.rearrange("p (s g i) -> p s g i", g=2, i=2),
+                                 diff[b, c][:].rearrange("p (g s i) -> p s g i", g=2, i=2), ABS)
 
         def quantise_gap(b, part, at=None):
             width = (HALF, CHUNK)[b]

@@ -120,11 +120,11 @@ def tile_list_map_change_gap_kernel(tc, tab_words, tab_scales, tab2_words, tab2_
         def round_on_gpsimd(dst, src):
             nc.gpsimd.tensor_scalar(dst, src, 1.0, 0.0, ALU.mult, ALU.add)
 
-        def round_w2(b, a, cast, at, part=slice(0, PACK)):
+        def round_w2(b, a, cast, at, part=slice(0, P)):
             if (b, a) not in w2_bf:
                 w2_bf[b, a] = tile("w2_bf%d%d" % (b, a), [P, PACK * PASS], BF16, at)
-            cast(w2_bf[b, a][:, PASS * part.start:PASS * part.stop].rearrange("p (t m j) -> p m t j", m=P, j=PACK),
-                 w2_raw[b, a][:].rearrange("p j (m t) -> p m t j", t=PACK)[:, :, part, :])
+            cast(w2_bf[b, a][:].rearrange("p (t m j) -> p m t j", m=P, j=PACK)[:, part],
+                 w2_raw[b, a][:].rearrange("p j (m t) -> p m t j", t=PACK)[:, part])
 
         def quantise_w2(b, a, at=None):
             w2_codes[b, a] = tile("w2_codes%d%d" % (b, a), [P, PASS], U32, at)
@@ -269,8 +269,8 @@ def tile_list_map_change_gap_kernel(tc, tab_words, tab_scales, tab2_words, tab2_
         old_chunk(0, 0)
         magnitudes(0, 0)
         old_chunk(0, 1)
-        round_w2(1, 1, nc.scalar.copy, area_e, slice(0, PACK // 2))
-        round_w2(1, 1, round_on_gpsimd, area_e, slice(PACK // 2, PACK))
+        round_w2(1, 1, nc.scalar.copy, area_e, slice(0, P // 2))
+        round_w2(1, 1, round_on_gpsimd, area_e, slice(P // 2, P))
         magnitudes(0, 1)
         old_chunk(0, 2)
         magnitudes(0, 2, area_b + 8 * KB)

@@ -315,5 +315,9 @@ def tile_list_map_change_gap_kernel(tc, tab_words, tab_scales, tab2_words, tab2_
         magnitude_and_store(2, 0)
         weigh_and_store(2, 1, nc.vector)
         magnitude_of_bank(3, 0)
-        weigh_and_store(3, 0, nc.vector)
-        magnitude_and_store(3, 1)
+        for i in range(2):
+            last = [tile("last%d%d" % (g, i), [P, CHUNK], F32) for g in range(2)]
+            nc.vector.tensor_tensor(last[0][:], halfway[3, 0][:, list_cols(i)], tw_sb[0][:, i, list_cols(3)], ALU.mult)
+            nc.scalar.activation(last[1][:], halfway[3, 1][:, list_cols(i)], ABS)
+            for g, queue in enumerate((nc.sync, nc.scalar)):
+                queue.dma_start(out[P * (2 * g + i):P * (2 * g + i + 1), list_cols(3)], last[g][:])

@@ -42,7 +42,8 @@ def tile_list_map_change_gap_kernel(tc, tab_words, tab_scales, tab2_words, tab2_
         def bank(index, name):
             return psum.tile([P, 2 * CHUNK], F32, name=name, tag="bank%d" % index, bufs=1)
 
-        area_a, area_b, area_c, area_d, area_f, area_e = 0, 16 * KB, 32 * KB, 40 * KB, 44 * KB, 48 * KB
+        area_a, area_b, area_c, area_d, area_f, area_e = 0, 8 * KB, 32 * KB, 40 * KB, 44 * KB, 48 * KB
+        area_g = 24 * KB
 
         list1 = keep.tile([P, S // 16], U16, name="list1")
         list2 = keep.tile([P, S // 16], U16, name="list2")
@@ -73,9 +74,8 @@ def tile_list_map_change_gap_kernel(tc, tab_words, tab_scales, tab2_words, tab2_
             for r in which:
                 nc.sync.dma_start(plane[r:P:32, :].bitcast(I32), rows[first + r:first + ROWS:4, :].bitcast(I32))
 
-        def deal_w4(dst, src):
-            nc.vector.tensor_copy(dst.rearrange("p (b t m) -> p b t m", b=2, t=PACK),
-                                  src.rearrange("p (b m t) -> p b t m", b=2, t=PACK))
+        def deal_w4(copy, dst, src):
+            copy(dst.rearrange("p (b t m) -> p b t m", b=2, t=PACK), src.rearrange("p (b m t) -> p b t m", b=2, t=PACK))
 
         w4_rows = tile("w4_rows", [P, H], U8)
         load_rows(w4_rows, w4_scales, P - ROWS)
@@ -85,7 +85,7 @@ def tile_list_map_change_gap_kernel(tc, tab_words, tab_scales, tab2_words, tab2_
         tab_rows = tile("tab_rows", [P, T], U8)
         load_rows(tab_rows, tab_scales, P - ROWS)
         nc.sync.dma_start(list2[:], offs2)
-        tab2_rows = tile("tab2_rows", [P, T], U8, area_c)
+        tab2_rows = tile("tab2_rows", [P, T], U8, area_c - 2 * KB)
         load_rows(tab2_rows, tab2_scales, 2 * ROWS)
         load_w2(0, 0, None)
         tab_w = tile("tab_w", [P, T], U32, area_b)
@@ -98,21 +98,21 @@ def tile_list_map_change_gap_kernel(tc, tab_words, tab_scales, tab2_words, tab2_
             nc.vector.memset(plane[:].bitcast(I32), 0)
 
         scan_rows = tile("scan_rows", [P, S + H], U8)
-        deal_w4(scan_rows[:, S:S + H], w4_rows[:])
+        deal_w4(nc.vector.tensor_copy, scan_rows[:, S:S + H], w4_rows[:])
         w4_w = tile("w4_w", [P, H], U16)
-        deal_w4(w4_w[:], w4_raw[:])
-        v_rows = tile("v_rows", [P, S], U8, area_a + 8 * KB - S // 2)
+        deal_w4(nc.scalar.copy, w4_w[:], w4_raw[:])
+        v_rows = tile("v_rows", [P, S], U8, area_a)
         nc.vector.tensor_copy(v_rows[:], tab_rows[:].indirect(list1[:]))
         nc.vector.tensor_copy(scan_rows[:, 0:S].bitcast(I32), v_rows[:].bitcast(I32))
         move_rows(scan_planes, scan_rows, P - ROWS)
         load_tab2(0, area_a)
-        load_w2(0, 1, area_a + 8 * KB)
 
         v2_rows = tile("v2_rows", [P, S], U8)
         nc.vector.tensor_copy(v2_rows[:], tab2_rows[:].indirect(list2[:]))
         move_rows(v2_planes[0], v2_rows, 2 * ROWS, range(2))
-        load_tab2(1, area_c)
+        load_w2(0, 1, area_g)
         move_rows(v2_planes[0], v2_rows, 2 * ROWS, range(2, QUADRANTS))
+        load_tab2(1, area_c)
         move_rows(v2_planes[1], v2_rows, 3 * ROWS)
 
         w2_bf, w2_codes, w2_sc = {}, {}, {}
@@ -152,7 +152,7 @@ def tile_list_map_change_gap_kernel(tc, tab_words, tab_scales, tab2_words, tab2_
         for q in range(QUADRANTS):
             nc.sync.dma_start(w8_sc[32 * q:32 * q + 8, :].bitcast(I32), w8_scales[:, 4 * q:4 * q + 4, :].bitcast(I32))
         round_w2(0, 1, nc.vector.tensor_copy, area_f)
-        load_tw(0, area_a + 8 * KB)
+        load_tw(0, area_g)
         quantise_w2(0, 1)
         for h in range(2):
             v2_w[1, h] = gather_half(tile("v2_w1%d" % h, [P, HALF], U16, area_f + KB * h), tab2_w[1], list2, h)
@@ -160,9 +160,9 @@ def tile_list_map_change_gap_kernel(tc, tab_words, tab_scales, tab2_words, tab2_
 
         scan_sb, diff, gap, gap_codes, gap_sc, y_ps, halfway = {}, {}, {}, {}, {}, {}, {}
         scan_at = {(0, 1, 1): area_e, (0, 3, 0): area_e + 4 * KB, (0, 3, 1): area_e + 6 * KB}
-        old_banks = ((5, 6, 7, 1, 2, 3, 4, 2), (5, 6, 7, 1, 0, 3, 4, 2))
+        old_banks = ((5, 6, 7, 1, 2, 3, 4, 2), (5, 6, 7, 1, 0, 3, 7, 1))
 
-        y_banks = (4, 2, 5, 6, 7, 1, 0, 3)
+        y_banks = (4, 2, 5, 6, 4, 2, 0, 3)
 
         def half_cols(c):
             return slice(CHUNK * (c % 2), CHUNK * (c % 2 + 1))

@@ -151,7 +151,9 @@ def tile_list_map_change_gap_kernel(tc, tab_words, tab_scales, tab2_words, tab2_
         nc.vector.memset(w8_sc[:].bitcast(I32), 0)
         for q in range(QUADRANTS):
             nc.sync.dma_start(w8_sc[32 * q:32 * q + 8, :].bitcast(I32), w8_scales[:, 4 * q:4 * q + 4, :].bitcast(I32))
-        round_w2(0, 1, nc.vector.tensor_copy, area_f)
+        w2_bf[0, 1] = tile("w2_bf01", [P, PACK * PASS], BF16, area_f)
+        nc.vector.tensor_copy(w2_bf[0, 1][:].rearrange("p (t m j) -> p m j t", m=P, j=PACK),
+                              w2_raw[0, 1][:].rearrange("p j (m t) -> p m j t", t=PACK))
         load_tw(0, area_g)
         quantise_w2(0, 1)
         for h in range(2):

@@ -199,6 +199,12 @@ def tile_list_map_change_gap_kernel(tc, tab_words, tab_scales, tab2_words, tab2_
             nc.vector.tensor_tensor(diff[b, c][:, 2 * CHUNK * g:2 * CHUNK * (g + 1)].rearrange("p (s i) -> p s i", i=2),
                                     woven(acc), scan_sb[b, c, g][:].rearrange("p (s i) -> p s i", i=2), ALU.subtract)
 
+        def keep_warm(index, passes):
+            idle = bank(index, "warm_ps")
+            for step in range(passes):
+                nc.tensor.matmul_mx(out=idle[:], lhsT=w2_codes[0, 0][:, 0:P].bitcast(FP8X4), lhsT_scale=w2_sc[0, 0][:, 0:P],
+                                    rhs=w2_codes[0, 0][:].bitcast(FP8X4), rhs_scale=w2_sc[0, 0][:], start=True, stop=True)
+
         def old_chunk(b, c, first_pass=1, at=None):
             for g in range(2):
                 old_bank(b, c, g, first_pass, at)
@@ -280,6 +286,9 @@ def tile_list_map_change_gap_kernel(tc, tab_words, tab_scales, tab2_words, tab2_
         quantise_w2(1, 0, area_e + 4 * KB)
         old_bank(0, 3, 1, 1)
         magnitudes(0, 3)
+        keep_warm(3, 1)
+        keep_warm(4, 1)
+        keep_warm(2, 2)
         quantise_w2(1, 1, area_e + 6 * KB)
         quantise_gap(0, 0, area_e + 2 * KB)
         old_chunk(1, 0, 0)

@@ -164,7 +164,7 @@ def tile_list_map_change_gap_kernel(tc, tab_words, tab_scales, tab2_words, tab2_
         scan_at = {(0, 1, 1): area_e, (0, 3, 0): area_e + 4 * KB, (0, 3, 1): area_e + 6 * KB}
         old_banks = ((5, 6, 7, 1, 2, 3, 4, 2), (5, 6, 7, 1, 0, 3, 7, 1))
 
-        y_banks = (4, 2, 5, 6, 4, 2, 0, 3)
+        y_banks = (4, 2, 5, 6, 7, 1, 0, 6)
 
         def half_cols(c):
             return slice(CHUNK * (c % 2), CHUNK * (c % 2 + 1))

from contextlib import ExitStack

import concourse.mybir as mybir

K, K2, H, N, T, S = 512, 1024, 1024, 512, 4096, 1024
FLOPS = 2 * S * (K * H + K2 * H + H * N)

F32 = mybir.dt.float32
BF16 = mybir.dt.bfloat16
I32 = mybir.dt.int32
U32 = mybir.dt.uint32
U16 = mybir.dt.uint16
U8 = mybir.dt.uint8
FP8X4 = mybir.dt.float8_e4m3fn_x4
FP4X4 = mybir.dt.float4_e2m1fn_x4
ALU = mybir.AluOpType
ABS = mybir.ActivationFunctionType.Abs

P = 128
PACK = 4
PASS = P * PACK
QUADRANTS = 4
ROWS = 16
HALF = S // 2
CHUNK = S // 4
KB = 1024


def tile_list_map_change_gap_kernel(tc, tab_words, tab_scales, tab2_words, tab2_scales, offs, offs2,
                                                 w4_words, w4_scales, w2, w8_words, w8_scales, tw, out):
    nc = tc.nc
    with ExitStack() as ctx:
        keep = ctx.enter_context(tc.tile_pool(name="keep", bufs=1))
        shared = ctx.enter_context(tc.tile_pool(name="shared", bufs=1))
        psum = ctx.enter_context(tc.psum_pool(name="psum", bufs=1))

        def tile(name, shape, dtype, at=None):
            if at is None:
                return keep.tile(shape, dtype, name=name, align_bytes=64)
            return shared.tile(shape, dtype, name=name, align_bytes=64, offset=at)

        def bank(index, name):
            return psum.tile([P, 2 * CHUNK], F32, name=name, tag="bank%d" % index, bufs=1)

        area_a, area_b, area_c, area_d, area_f, area_e = 0, 8 * KB, 32 * KB, 40 * KB, 44 * KB, 48 * KB
        area_g = 24 * KB

        list1 = keep.tile([P, S // 16], U16, name="list1")
        list2 = keep.tile([P, S // 16], U16, name="list2")
        w2_raw, tab2_w, tw_sb = {}, {}, {}

        def load_w2(b, a, at):
            w2_raw[b, a] = tile("w2_raw%d%d" % (b, a), [P, PACK, PASS], F32, at)
            nc.sync.dma_start(w2_raw[b, a][:], w2[PASS * a:PASS * (a + 1), PASS * b:PASS * (b + 1)].rearrange(
                "(p j) c -> p j c", j=PACK))

        def load_tab2(a, at):
            tab2_w[a] = tile("tab2_w%d" % a, [P, T], U16, at)
            nc.sync.dma_start(tab2_w[a][:].bitcast(I32), tab2_words[a].bitcast(I32))

        def load_tw(g, at):
            tw_sb[g] = tile("tw%d" % g, [P, 2, S], F32, at)
            nc.sync.dma_start(tw_sb[g][:], tw[2 * P * g:2 * P * (g + 1), :].rearrange("(i p) s -> p i s", p=P))

        def load_rows(rows_tile, scales, first):
            rows = scales.rearrange("a q c -> (a q) c")
            last = first + rows.shape[0]
            nc.sync.dma_start(rows_tile[first:last, :].bitcast(I32), rows.bitcast(I32))
            nc.vector.memset(rows_tile[0:first, :].bitcast(I32), 0)
            if last < P:
                nc.gpsimd.memset(rows_tile[last:P, :].bitcast(I32), 0)

        def move_rows(plane, rows, first, which=range(QUADRANTS)):
            for r in which:
                nc.sync.dma_start(plane[r:P:32, :].bitcast(I32), rows[first + r:first + ROWS:4, :].bitcast(I32))

        def deal_w4(copy, dst, src):
            copy(dst.rearrange("p (b t m) -> p b t m", b=2, t=PACK), src.rearrange("p (b m t) -> p b t m", b=2, t=PACK))

        w4_rows = tile("w4_rows", [P, H], U8)
        load_rows(w4_rows, w4_scales, P - ROWS)
        w4_raw = tile("w4_raw", [P, H], U16)
        nc.sync.dma_start(w4_raw[:].bitcast(I32), w4_words[0].bitcast(I32))
        nc.sync.dma_start(list1[:], offs)
        tab_rows = tile("tab_rows", [P, T], U8)
        load_rows(tab_rows, tab_scales, P - ROWS)
        nc.sync.dma_start(list2[:], offs2)
        tab2_rows = tile("tab2_rows", [P, T], U8, area_c - 2 * KB)
        load_rows(tab2_rows, tab2_scales, 2 * ROWS)
        load_w2(0, 0, None)
        tab_w = tile("tab_w", [P, T], U32, area_b)
        nc.sync.dma_start(tab_w[:].bitcast(I32), tab_words[0].rearrange("p t i -> p (t i)").bitcast(I32))

        scan_planes = tile("scan_planes", [P, S + H], U8)
        nc.vector.memset(scan_planes[:].bitcast(I32), 0)
        v2_planes = [tile("v2_plane%d" % a, [P, S], U8) for a in range(2)]
        for plane in v2_planes:
            nc.vector.memset(plane[:].bitcast(I32), 0)

        scan_rows = tile("scan_rows", [P, S + H], U8)
        deal_w4(nc.vector.tensor_copy, scan_rows[:, S:S + H], w4_rows[:])
        w4_w = tile("w4_w", [P, H], U16)
        deal_w4(nc.scalar.copy, w4_w[:], w4_raw[:])
        v_rows = tile("v_rows", [P, S], U8, area_a)
        nc.vector.tensor_copy(v_rows[:], tab_rows[:].indirect(list1[:]))
        nc.vector.tensor_copy(scan_rows[:, 0:S].bitcast(I32), v_rows[:].bitcast(I32))
        move_rows(scan_planes, scan_rows, P - ROWS)
        load_tab2(0, area_a)

        v2_rows = tile("v2_rows", [P, S], U8)
        nc.vector.tensor_copy(v2_rows[:], tab2_rows[:].indirect(list2[:]))
        move_rows(v2_planes[0], v2_rows, 2 * ROWS, range(2))
        load_w2(0, 1, area_g)
        move_rows(v2_planes[0], v2_rows, 2 * ROWS, range(2, QUADRANTS))
        load_tab2(1, area_c)
        move_rows(v2_planes[1], v2_rows, 3 * ROWS)

        w2_bf, w2_codes, w2_sc = {}, {}, {}

        def round_on_gpsimd(dst, src):
            nc.gpsimd.tensor_scalar(dst, src, 1.0, 0.0, ALU.mult, ALU.add)

        def round_w2(b, a, cast, at, part=slice(0, P)):
            if (b, a) not in w2_bf:
                w2_bf[b, a] = tile("w2_bf%d%d" % (b, a), [P, PACK * PASS], BF16, at)
            cast(w2_bf[b, a][:].rearrange("p (t m j) -> p m t j", m=P, j=PACK)[:, part],
                 w2_raw[b, a][:].rearrange("p j (m t) -> p m t j", t=PACK)[:, part])

        def quantise_w2(b, a, at=None):
            w2_codes[b, a] = tile("w2_codes%d%d" % (b, a), [P, PASS], U32, at)
            w2_sc[b, a] = tile("w2_sc%d%d" % (b, a), [P, PASS], U8)
            nc.vector.quantize_mx(out=w2_codes[b, a][:].bitcast(FP8X4), scales=w2_sc[b, a][:], in_=w2_bf[b, a][:])

        def gather_half(picked, window, offsets, h):
            nc.vector.tensor_copy(picked[:], window[:].indirect(offsets[:, h * HALF // 16:(h + 1) * HALF // 16]))
            return picked

        round_w2(0, 0, nc.scalar.copy, area_d)
        quantise_w2(0, 0)
        v_w = [gather_half(tile("v_w%d" % h, [P, HALF], U32, area_d + 2 * KB * h), tab_w, list1, h)
               for h in range(2)]
        for a in range(2):
            load_w2(1, a, area_b + 8 * KB * a)
        v2_w = {}
        for h in range(2):
            v2_w[0, h] = gather_half(tile("v2_w0%d" % h, [P, HALF], U16), tab2_w[0], list2, h)
        w8_w = tile("w8_w", [P, 2 * N], U32, area_a)
        nc.sync.dma_start(w8_w[:].bitcast(I32).rearrange("p (b c) -> p b c", b=2),
                          w8_words.rearrange("b p c i -> p b (c i)").bitcast(I32))
        w8_sc = tile("w8_sc", [P, N], U8, area_a + 4 * KB)
        nc.vector.memset(w8_sc[:].bitcast(I32), 0)
        for q in range(QUADRANTS):
            nc.sync.dma_start(w8_sc[32 * q:32 * q + 8, :].bitcast(I32), w8_scales[:, 4 * q:4 * q + 4, :].bitcast(I32))
        w2_bf[0, 1] = tile("w2_bf01", [P, PACK * PASS], BF16, area_f)
        nc.vector.tensor_copy(w2_bf[0, 1][:].rearrange("p (t m j) -> p m j t", m=P, j=PACK),
                              w2_raw[0, 1][:].rearrange("p j (m t) -> p m j t", t=PACK))
        load_tw(0, area_g)
        quantise_w2(0, 1)
        for h in range(2):
            v2_w[1, h] = gather_half(tile("v2_w1%d" % h, [P, HALF], U16, area_f + KB * h), tab2_w[1], list2, h)
        load_tw(1, area_c)

        scan_sb, diff, gap, gap_codes, gap_sc, y_ps, halfway = {}, {}, {}, {}, {}, {}, {}
        scan_at = {(0, 1, 1): area_e, (0, 3, 0): area_e + 4 * KB, (0, 3, 1): area_e + 6 * KB}
        old_banks = ((5, 6, 7, 1, 2, 3, 4, 2), (5, 6, 7, 1, 0, 3, 7, 1))

        y_banks = (4, 2, 5, 6, 7, 1, 0, 6)

        def half_cols(c):
            return slice(CHUNK * (c % 2), CHUNK * (c % 2 + 1))

        def list_cols(c):
            return slice(CHUNK * c, CHUNK * (c + 1))

        def woven(acc):
            return acc[:].rearrange("p (i s) -> p s i", i=2)

        def scan_bank(b, c, g):
            acc = bank((8 * b + 2 * c + g) % 5, "scan_ps")
            for i in range(2):
                col = PASS * b + P * (2 * g + i)
                nc.tensor.matmul_mx(out=acc[:, list_cols(i)], lhsT=w4_w[:, col:col + P].bitcast(FP4X4),
                                    lhsT_scale=scan_planes[:, S + col:S + col + P],
                                    rhs=v_w[c // 2][:, half_cols(c)].bitcast(FP8X4),
                                    rhs_scale=scan_planes[:, list_cols(c)], start=True, stop=True)
            scan_sb[b, c, g] = tile("scan%d%d%d" % (b, c, g), [P, 2 * CHUNK], F32, scan_at.get((b, c, g)))
            nc.scalar.copy(scan_sb[b, c, g][:].rearrange("p (s i) -> p s i", i=2), woven(acc))

        def old_bank(b, c, g, first_pass, at=None):
            if g == 0:
                diff[b, c] = tile("diff%d%d" % (b, c), [P, PACK * CHUNK], BF16, at)
            acc = bank(old_banks[b][2 * c + g], "old_ps")
            for step, (a, i) in enumerate((a, i) for a in (first_pass, 1 - first_pass) for i in range(2)):
                cols = slice(P * (2 * g + i), P * (2 * g + i + 1))
                nc.tensor.matmul_mx(out=acc[:, list_cols(i)], lhsT=w2_codes[b, a][:, cols].bitcast(FP8X4),
                                    lhsT_scale=w2_sc[b, a][:, cols],
                                    rhs=v2_w[a, c // 2][:, half_cols(c)].bitcast(FP4X4),
                                    rhs_scale=v2_planes[a][:, list_cols(c)], start=(step == 0), stop=(step == 3))
            nc.vector.tensor_tensor(diff[b, c][:, 2 * CHUNK * g:2 * CHUNK * (g + 1)].rearrange("p (s i) -> p s i", i=2),
                                    woven(acc), scan_sb[b, c, g][:].rearrange("p (s i) -> p s i", i=2), ALU.subtract)

        def keep_warm(index, passes):
            idle = bank(index, "warm_ps")
            for step in range(passes):
                nc.tensor.matmul_mx(out=idle[:], lhsT=w2_codes[0, 0][:, 0:P].bitcast(FP8X4), lhsT_scale=w2_sc[0, 0][:, 0:P],
                                    rhs=w2_codes[0, 0][:].bitcast(FP8X4), rhs_scale=w2_sc[0, 0][:], start=True, stop=True)

        def old_chunk(b, c, first_pass=1, at=None):
            for g in range(2):
                old_bank(b, c, g, first_pass, at)

        def magnitudes(b, c, at=None):
            if b == 1:
                gap[b, c] = tile("gap1%d" % c, [P, CHUNK * PACK], BF16, at)
                dst = gap[b, c][:]
            else:
                if c % 2 == 0:
                    gap[b, c // 2] = tile("gap0%d" % (c // 2), [P, HALF * PACK], BF16, at)
                dst = gap[b, c // 2][:, PACK * CHUNK * (c % 2):PACK * CHUNK * (c % 2 + 1)]
            nc.scalar.activation(dst.rearrange("p (s g i) -> p s g i", g=2, i=2),
                                 diff[b, c][:].rearrange("p (g s i) -> p s g i", g=2, i=2), ABS)

        def quantise_gap(b, part, at=None):
            width = (HALF, CHUNK)[b]
            gap_codes[b, part] = tile("gap_codes%d%d" % (b, part), [P, width], U32, at)
            gap_sc[b, part] = tile("gap_sc%d%d" % (b, part), [P, width], U8)
            nc.vector.quantize_mx(out=gap_codes[b, part][:].bitcast(FP8X4), scales=gap_sc[b, part][:],
                                  in_=gap[b, part][:])

        def y_passes(c, b):
            part, cols = ((c // 2, half_cols(c)), (c, slice(0, CHUNK)))[b]
            for g in range(2):
                if b == 0:
                    y_ps[c, g] = bank(y_banks[2 * c + g], "y_ps")
                for i in range(2):
                    col = P * (2 * g + i)
                    nc.tensor.matmul_mx(out=y_ps[c, g][:, list_cols(i)],
                                        lhsT=w8_w[:, N * b + col:N * b + col + P].bitcast(FP8X4),
                                        lhsT_scale=w8_sc[4 * b:P, col:col + P],
                                        rhs=gap_codes[b, part][:, cols].bitcast(FP8X4),
                                        rhs_scale=gap_sc[b, part][:, cols],
                                        start=(b == 0 and i == 0), stop=(b == 1 and i == 1))

        def pair_view(ap):
            return ap.rearrange("p (i s) -> p i s", i=2)

        def store(c, g, res):
            nc.sync.dma_start(out[2 * P * g:2 * P * (g + 1), list_cols(c)].rearrange("(i p) s -> p i s", p=P),
                              pair_view(res[:]))

        def tw_cols(c, g):
            return tw_sb[g][:, :, list_cols(c)]

        def weigh_bank(c, g):
            halfway[c, g] = tile("weighted%d%d" % (c, g), [P, 2 * CHUNK], F32)
            nc.vector.tensor_tensor(pair_view(halfway[c, g][:]), pair_view(y_ps[c, g][:]), tw_cols(c, g), ALU.mult)

        def magnitude_and_store(c, g):
            res = tile("res%d%d" % (c, g), [P, 2 * CHUNK], F32)
            nc.scalar.activation(res[:], halfway[c, g][:], ABS)
            store(c, g, res)

        def magnitude_of_bank(c, g, at=None):
            halfway[c, g] = tile("size%d%d" % (c, g), [P, 2 * CHUNK], F32, at)
            nc.scalar.activation(halfway[c, g][:], y_ps[c, g][:], ABS)

        def weigh_and_store(c, g, engine, at=None):
            res = tile("res%d%d" % (c, g), [P, 2 * CHUNK], F32, at)
            engine.tensor_tensor(pair_view(res[:]), pair_view(halfway[c, g][:]), tw_cols(c, g), ALU.mult)
            store(c, g, res)

        for b in range(2):
            for c in range(4):
                for g in range(2):
                    scan_bank(b, c, g)
        round_w2(1, 0, round_on_gpsimd, None)
        old_chunk(0, 0)
        magnitudes(0, 0)
        old_chunk(0, 1)
        round_w2(1, 1, nc.scalar.copy, area_e, slice(0, P // 2))
        round_w2(1, 1, round_on_gpsimd, area_e, slice(P // 2, P))
        magnitudes(0, 1)
        old_chunk(0, 2)
        magnitudes(0, 2, area_b + 8 * KB)
        old_bank(0, 3, 0, 1)
        quantise_w2(1, 0, area_e + 4 * KB)
        old_bank(0, 3, 1, 1)
        magnitudes(0, 3)
        keep_warm(3, 1)
        keep_warm(4, 1)
        keep_warm(2, 2)
        quantise_w2(1, 1, area_e + 6 * KB)
        quantise_gap(0, 0, area_e + 2 * KB)
        old_chunk(1, 0, 0)
        magnitudes(1, 0)
        old_chunk(1, 1)
        magnitudes(1, 1, area_e + 8 * KB)
        y_passes(0, 0)
        quantise_gap(1, 0)
        y_passes(0, 1)
        quantise_gap(0, 1)
        quantise_gap(1, 1)
        old_chunk(1, 2, 1, area_e + 8 * KB)
        y_passes(1, 0)
        y_passes(1, 1)
        magnitude_of_bank(0, 0)
        weigh_and_store(0, 0, nc.gpsimd)
        magnitude_of_bank(0, 1, area_e + 10 * KB)
        weigh_and_store(0, 1, nc.gpsimd)
        magnitude_of_bank(1, 0)
        magnitudes(1, 2)
        old_chunk(1, 3)
        magnitudes(1, 3)
        weigh_bank(1, 1)
        quantise_gap(1, 2, area_e + 10 * KB)
        y_passes(2, 0)
        y_passes(2, 1)
        weigh_and_store(1, 0, nc.vector, area_e + 11 * KB)
        quantise_gap(1, 3)
        y_passes(3, 0)
        y_passes(3, 1)
        magnitude_and_store(1, 1)
        weigh_bank(2, 0)
        magnitude_of_bank(2, 1)
        weigh_bank(3, 1)
        magnitude_and_store(2, 0)
        weigh_and_store(2, 1, nc.vector)
        magnitude_of_bank(3, 0)
        for i in range(2):
            last = [tile("last%d%d" % (g, i), [P, CHUNK], F32) for g in range(2)]
            nc.vector.tensor_tensor(last[0][:], halfway[3, 0][:, list_cols(i)], tw_sb[0][:, i, list_cols(3)], ALU.mult)
            nc.scalar.activation(last[1][:], halfway[3, 1][:, list_cols(i)], ABS)
            for g, queue in enumerate((nc.sync, nc.scalar)):
                queue.dma_start(out[P * (2 * g + i):P * (2 * g + i + 1), list_cols(3)], last[g][:])
